import numpy as np, ml_dtypes
CORES = [10,34,74,98]
N = 4
BF = ml_dtypes.bfloat16
def f(rng, *shape):
    return (rng.standard_normal(shape, dtype=np.float32) * np.exp2(rng.integers(-2, 3, shape[:-1] + (1,)))).astype(BF)
def wide(rng, *shape):
    v = f(rng, *shape).astype(np.float32); k = shape[:-2] + (1, shape[-1])
    return (v * np.exp2(rng.integers(-6, 7, k)) * (rng.random(k) > 0.0625)).astype(BF)
def gentries(a):
    return np.ascontiguousarray(a.reshape(8, 16, -1).transpose(0, 2, 1)).reshape(8, -1)
def gtable(e):
    e = np.asarray(e); return np.ascontiguousarray(e.reshape(8, -1, 16).transpose(0, 2, 1)).reshape(128, -1).astype(np.int32)
B, M, W, S = 32, 128, 16, 2176
WL, WM, CB, CW = 4, 12, 6, 368
D, FR = 4096, 16
MB = M // 16
U, UB = CW // MB, S // MB
def book(rng, v):
    return (v.astype(np.float32) * (1 + rng.random(v.shape, dtype=np.float32))).astype(BF)
def parts(rng, k, s, exact):
    v = rng.integers(WL, WM + 1, k); t = s if exact else min(s, int(np.sum(v)))
    while np.sum(v) != t:
        e = 1 if np.sum(v) < t else -1
        i = np.flatnonzero(v < WM) if e > 0 else np.flatnonzero(v > WL)
        v[rng.permutation(i)[:abs(t - int(np.sum(v)))]] += e
    return v
def widths(rng):
    w = np.zeros((N, 8, B), np.int64)
    for q in range(N):
        for g in range(8):
            w[q, g] = parts(rng, B, UB, False); w[q, g, rng.integers(B)] = WL
    return w
def pick(rng, w, c, cand):
    left = U; lo = int(np.min(w[cand])); out = []
    for i in range(c):
        ok = cand[w[cand] <= left - (c - 1 - i) * lo]
        b = int(ok[rng.integers(len(ok))]); out.append(b); left -= int(w[b])
    return out
def wants(rng, w, uneven=False, full=None):
    L = np.zeros((N, 8, W), np.int64)
    for r in range(N):
        for g in range(8):
            q0 = -1
            own = np.repeat(rng.permutation(N), CB)
            if not uneven: own = rng.permutation(own)
            if full is not None:
                q0 = (r + 1 + g % (N - 1)) % N
                own = np.concatenate([np.full(CB, q0), own[own != q0]])
            c = np.bincount(own[:W], minlength=N); e = []
            for q in range(N):
                if q == q0:
                    e += [q * B + int(b) for b in full[q, g]]
                elif c[q]:
                    cand = np.arange(B)
                    if uneven and rng.random() < 0.5: cand = np.array([int(np.argmin(w[q, g])), int(rng.integers(B))])
                    e += [q * B + b for b in pick(rng, w[q, g], int(c[q]), cand)]
            L[r, g] = rng.permutation(np.array(e))
    return L
def make(rng, w, L, s):
    return {"strm": s.astype(np.int32), "wd": np.stack([gtable(u) for u in w]), "want": np.stack([gtable(u) for u in L]), "dic": book(rng, f(rng, N, 8 * FR, D))}
def setup_inputs(rng):
    w = widths(rng)
    return make(rng, w, wants(rng, w), rng.integers(0, 65536, (N, 8, S)))
def setup_inputs_full(rng):
    w = np.zeros((N, 8, B), np.int64); full = np.zeros((N, 8, CB), np.int64)
    for q in range(N):
        for g in range(8):
            p = np.concatenate([np.array([0, B - 1]), rng.permutation(np.arange(1, B - 1))])
            w[q, g, p[:CB]] = parts(rng, CB, U, True); w[q, g, p[CB:]] = parts(rng, B - CB, UB - U, True); full[q, g] = p[:CB]
    return make(rng, w, wants(rng, w, full=full), rng.integers(0, 65536, (N, 8, S)))
def setup_inputs_uneven(rng):
    w = widths(rng)
    return make(rng, w, wants(rng, w, uneven=True), rng.integers(0, 65536, (N, 8, S)))
def setup_inputs_ends(rng):
    w = np.full((N, 8, B), WL, np.int64); most = min(B - 1, (UB - B * WL) // (WM - WL))
    for q in range(N):
        for g in range(8):
            w[q, g, rng.permutation(B)[:rng.integers(0, most + 1)]] = WM
    s = rng.choice(np.array([0, 0, 1, 32768, 65535, 65535]), (N, 8, S))
    s = np.where(rng.random((N, 8, S)) < 0.25, rng.integers(0, 65536, (N, 8, S)), s)
    return make(rng, w, wants(rng, w), s)
def setup_inputs_spread(rng):
    d = setup_inputs(rng); d["dic"] = book(rng, wide(rng, N, 8 * FR, D)); return d
def check_inputs(d):
    try:
        bad = []
        if d["strm"].min() < 0 or d["strm"].max() > 65535: bad.append("words")
        if not np.isfinite(d["dic"].astype(np.float32)).all(): bad.append("finite")
        w = np.stack([gentries(u) for u in d["wd"]]).astype(np.int64); L = np.stack([gentries(u) for u in d["want"]]).astype(np.int64)
        if w.min() < WL or w.max() > WM: bad.append("widths")
        if (MB * np.sum(w, axis=2) > S).any(): bad.append("words of a column")
        if L.min() < 0 or L.max() >= N * B: return bad + ["wanted blocks"]
        n = np.zeros((N, 8, N), np.int64); m = np.zeros((N, 8, N), np.int64)
        for r in range(N):
            for g in range(8):
                q, b = L[r, g] // B, L[r, g] % B
                np.add.at(n[r, g], q, 1); np.add.at(m[r, g], q, MB * w[q, g, b])
        if n.max() > CB: bad.append("blocks of a pair")
        if m.max() > CW: bad.append("words of a pair")
        return bad
    except Exception:
        return ["shapes"]
def reference(strm, wd, want, dic):
    y = np.zeros((N, 8 * FR, W * M), dic.dtype)
    bit = (strm.astype(np.int64)[..., None] >> np.arange(16) & 1).reshape(N, 8, 16 * S)
    w = np.stack([gentries(wd[q]) for q in range(N)]).astype(np.int64)
    first = M * (np.add.accumulate(w, axis=2) - w)
    for r in range(N):
        L = gentries(want[r]).astype(np.int64)
        for g in range(8):
            q, b = L[g] // B, L[g] % B
            v = w[q, g, b][:, None]; at = first[q, g, b][:, None] + np.arange(M) * v
            code = np.zeros((W, M), np.int64)
            for k in range(WM):
                code += np.where(k < v, bit[q[:, None], g, np.minimum(at + k, 16 * S - 1)], 0) << k
            y[r, FR * g:FR * (g + 1)] = dic[r, FR * g:FR * (g + 1)][:, code.reshape(-1)]
    return {"y": y}

@@ -1,0 +1,305 @@
+from concourse.bass import DstId, RemoteDMATransfer
+from concourse.mybir import AluOpType, AxisListType, ActivationFunctionType
+
+N = 4
+S = 2176
+HB = 512
+WN = S - HB
+H0 = 1536
+ZB = 40
+ZZ = 3 * ZB
+RND = 402653184.0
+D0 = 1536
+
+F, I, U, BF = "float32", "int32", "uint16", "bfloat16"
+SCRATCH = {
+    "win": ("sbuf", [128, WN], I), "dc": ("sbuf", [128, 4096], BF), "ob": ("sbuf", [128, 2048], BF),
+    "wt": ("sbuf", [128, 1], I), "wdi": ("sbuf", [128, 2], I), "wdu": ("sbuf", [128, 4], U),
+    "wout": ("dram", [128, 2], I), "win4": ("dram", [N, 128, 2], I), "wall": ("sbuf", [128, 2 * N], I), "walu": ("sbuf", [128, 2 * N], U),
+    "pi": ("sbuf", [128, 1], I), "bi": ("sbuf", [128, 4], I), "bf": ("sbuf", [128, 4], F),
+    "ev": ("sbuf", [128, 1], F), "pev": ("sbuf", [128, 1], F),
+    "i16": ("sbuf", [128, 16], F), "tabq": ("sbuf", [128, 128], F), "isl": ("sbuf", [128, 128], F),
+    "eh": ("sbuf", [128, 40], F), "ua": ("sbuf", [128, 32], F), "ub": ("sbuf", [128, 32], F), "utab": ("sbuf", [128, 128], F),
+    "qc": ("sbuf", [128, 12], F), "t2": ("sbuf", [128, 12], BF), "one": ("sbuf", [128, 128], BF),
+    "tri": ("sbuf", [128, 16], F), "diag": ("sbuf", [128, 16], F),
+    "wu": ("sbuf", [128, 2], U), "qk": ("sbuf", [128, 1], F), "q32": ("sbuf", [128, 1], F),
+    "z": ("sbuf", [128, 16], F), "eq": ("sbuf", [128, 17], F), "rk": ("sbuf", [128, 1], F),
+    "ud": ("sbuf", [128, 16], F), "u": ("sbuf", [128, 1], F),
+    "lh": ("sbuf", [128, 128], BF), "rh": ("sbuf", [128, 12], BF),
+    "msg": ("sbuf", [128, N, 4], U), "req": ("sbuf", [128, N, 4], U),
+    "tab8": ("sbuf", [128, 16], F), "o32": ("sbuf", [128, 32], F),
+    "ta": ("sbuf", [128, 16], I), "tb": ("sbuf", [128, 16], I), "tab2": ("sbuf", [128, 16], F),
+    "w8": ("sbuf", [128, 32], F), "dx": ("sbuf", [128, 32], F), "inc": ("sbuf", [128, 32], F), "xs": ("sbuf", [128, 32], F),
+    "o1": ("sbuf", [128, 32], U),
+    "gw": ("sbuf", [128, 528], F), "tw": ("sbuf", [128, 1024], F),
+    "rsp": ("sbuf", [128, N, 48], U), "ans": ("sbuf", [128, N, 48], U), "rf": ("sbuf", [128, 200], F),
+    "hf": ("sbuf", [128, ZB], F), "zr": ("sbuf", [128, ZB], F), "pw": ("sbuf", [128, ZB], F),
+    "pt": ("sbuf", [128, 2 * ZZ + 8], F), "pa": ("sbuf", [128, ZZ], F), "pb": ("sbuf", [128, ZZ], F),
+    "c16": ("sbuf", [128, 16], F), "ab8": ("sbuf", [128, 16], F), "ab40": ("sbuf", [128, 16], F),
+    "wrep": ("sbuf", [128, 128], F), "wdg": ("sbuf", [128, 16], F), "wi": ("sbuf", [128, 1], F),
+    "wii": ("sbuf", [128, 1], I), "woi": ("sbuf", [128, 1], I), "zo": ("sbuf", [128, 1], F), "sq": ("sbuf", [128, 1], F),
+    "cw": ("sbuf", [128, 16], I), "po": ("sbuf", [128, 16], I), "fo": ("sbuf", [128, 16], I),
+    "j1": ("sbuf", [128, 16], F), "j2": ("sbuf", [128, 16], F), "ab8s": ("sbuf", [128, 16], F),
+    "x1": ("sbuf", [128, 16], U), "x2": ("sbuf", [128, 8], U), "x3": ("sbuf", [128, 8], U), "o2": ("sbuf", [128, 16], U),
+    "m1": ("sbuf", [128, 256], F), "m2": ("sbuf", [128, 256], F),
+    "ya": ("sbuf", [128, 256], I), "yb": ("sbuf", [128, 256], I), "yc": ("sbuf", [128, 128], F), "yd": ("sbuf", [128, 128], F),
+    "cu": ("sbuf", [128, 128], U),
+    "ps": ("psum", [128, 512], F), "pm": ("psum", [128, 512], F), "pc": ("psum", [128, 512], F),
+}
+NS = 128
+SEMAPHORES = (["s%d" % k for k in range(NS)] + ["rq%d" % k for k in range(N)] + ["an%d" % k for k in range(N)]
+              + ["wq", "lw", "lq", "la", "gq", "ga"])
+
+A = AluOpType
+X = AxisListType.X
+COPY = ActivationFunctionType.Copy
+IDENT = ActivationFunctionType.Identity
+
+
+def emit(ops, queues, T):
+    last, readers, deps = {}, {}, []
+    for n, o in enumerate(ops):
+        d = set()
+        for k in o["r"]:
+            d.update(last.get(k, []))
+        for k in o["w"]:
+            if not (o["grp"] and all(ops[m]["grp"] == o["grp"] for m in last.get(k, []))):
+                d.update(last.get(k, []))
+                last[k] = []
+            d.update(readers.get(k, []))
+            readers[k] = []
+        for k in o["r"]:
+            readers.setdefault(k, []).append(n)
+        for k in o["w"]:
+            last.setdefault(k, []).append(n)
+        d.discard(n)
+        deps.append(d)
+    key = [o["grp"] or ("op", n) for n, o in enumerate(ops)]
+    need = set(key[m] for d in deps for m in d)
+    total, sem = {}, {}
+    for n, o in enumerate(ops):
+        if key[n] in need:
+            total[key[n]] = total.get(key[n], 0) + o["inc"]
+            if key[n] not in sem:
+                sem[key[n]] = T.sem["s%d" % len(sem)]
+    done = {}
+    for n, o in enumerate(ops):
+        q = queues[o["q"]]
+        seen = done.setdefault(o["q"], set())
+        for k in sorted(set(key[m] for m in deps[n]), key=str):
+            if k not in seen and total[k]:
+                q.wait_ge(sem[k], total[k])
+                seen.add(k)
+        for s, v in o["ext"]:
+            if s not in seen:
+                q.wait_ge(T.sem[s], v)
+                seen.add(s)
+        ins = o["f"](q)
+        if key[n] in need and o["inc"]:
+            ins.then_inc(sem[key[n]], o["inc"])
+
+
+def rank_program(g, core, T, topo):
+    me = T.rank_of(core)
+    if me is None:
+        return
+
+    def near(a, b):
+        return topo.same_plane(topo.chip(T.cores[a]), topo.chip(T.cores[b]))
+
+    steps = sorted(range(1, N), key=lambda d: sum(near(r, (r + d) % N) for r in range(N)))
+    ask = [(me + d) % N for d in steps]
+    tell = [(me - d) % N for d in steps]
+    ops = []
+
+    def op(q, f, r, w, grp=None, inc=1, ext=()):
+        ops.append({"q": q, "f": f, "r": list(r), "w": list(w), "grp": grp, "inc": inc, "ext": list(ext)})
+
+    def ts(out, in0, s1, s2, o0, o1, r, w, **kw):
+        if o1 is None:
+            op("v", lambda q: q.tensor_scalar(out, in0, s1, None, o0), r, w, **kw)
+        else:
+            op("v", lambda q: q.tensor_scalar(out, in0, s1, s2, o0, o1), r, w, **kw)
+
+    def tt(out, a, b, o, r, w, **kw):
+        op("v", lambda q: q.tensor_tensor(out, a, b, o), r, w, **kw)
+
+    def cp(out, a, r, w, **kw):
+        op("v", lambda q: q.tensor_copy(out, a), r, w, **kw)
+
+    def ms(out, c, w, **kw):
+        op("v", lambda q: q.memset(out, c), [], w, **kw)
+
+    def red(out, a, r, w):
+        op("v", lambda q: q.tensor_reduce(out, a, X, A.add), r, w)
+
+    def act(out, a, r, w, f=COPY, grp=None, **kw):
+        op("a", lambda q: q.activation(out, a, f, **kw), r, w, grp=grp)
+
+    def dma(qn, out, a, r, w, **kw):
+        op(qn, lambda q: q.dma_start(out, a), r, w, inc=16, **kw)
+
+    def iota(out, pat, base, cm, w, flt=True):
+        if flt:
+            op("g", lambda q: q.iota(out, pat, base, cm, allow_small_or_imprecise_dtypes=True), [], w)
+        else:
+            op("g", lambda q: q.iota(out, pat, base, cm), [], w)
+
+    def send(src, dst, sem, local, p, r):
+        rid, pid, _ = topo.addr(T.cores[p])
+        op("g", lambda q: q.remote_dma(dst, src, T.sem["%s%d" % (sem, me)], T.sem[local], pid, rid,
+                                       topo.mask(core, T.cores[p])), r, [], inc=0)
+        return len(topo.engines(core, T.cores[p]))
+
+    def arrivals(p):
+        return len(topo.engines(T.cores[p], core))
+
+    p16, od, kk, pod = T.bf[:, 0:1], T.bf[:, 1:2], T.bf[:, 2:3], T.bf[:, 3:4]
+
+    ms(T.win[:, H0:WN], 0, ["wtail"])
+    dma("a", T.wout[:], T.wd[:], [], ["wout"])
+    dma("s", T.wt[:], T.want[:], [], ["wt"])
+    dma("a", T.wdi[:], T.wd[:], [], ["wdi"])
+    for k in range(8):
+        dma("sa"[k % 2], T.win[k::16, 0:H0], T.strm[:, k:k + H0], [], ["win"], grp="win")
+    for k in range(8):
+        dma("as"[k < 5], T.win[8 + k::16, 0:WN - k], T.strm[:, HB + k:S], ["wtail"], ["win"], grp="win")
+
+    iota(T.pi[:], [[0, 1]], 0, 1, ["pi"], flt=False)
+    iota(T.i16[:], [[1, 16]], 0, 0, ["i16"])
+    iota(T.eh[:, 8:40], [[33, 2], [4, 8], [64, 2]], 0, 0, ["eh"])
+    iota(T.tabq[:], [[32, 4], [0, 32]], 0, 0, ["tabq"])
+    iota(T.qc[:], [[32, 4], [0, 3]], 0, 0, ["qc"])
+    iota(T.isl[:], [[16, 8], [0, 2], [1, 8]], 0, 0, ["isl"])
+    iota(T.t2[0:1, :], [[0, 4], [2, 3]], 0, 0, ["t2"])
+
+    far = [topo.addr(T.cores[p]) for p in ask]
+    wtr = RemoteDMATransfer(dst_ids=[DstId(rid=a[0], pnc=a[1]) for a in far], dma_engine_mask=topo.mask(core, T.cores[ask[0]]),
+                            remote_sem=T.sem.wq, srcs=[T.wout[:]], dsts=[T.win4[me] for _ in far])
+    op("g", lambda q: q.remote_dma_fused([wtr], local_sem=T.sem.lw), ["wout"], [], inc=0)
+    nw = len(topo.engines(core, T.cores[ask[0]]))
+
+    act(T.tab8[:], T.i16[:], ["i16"], ["tab8"], f=IDENT, scale=8.0)
+    ms(T.one[0:1, :], 1.0, ["one"])
+    ms(T.eh[:, 7:8], 124.0, ["eh0"])
+    ts(T.bi[:, 0:1], T.pi[:], 15, None, A.bitwise_and, None, ["pi"], ["bi"], grp="bi")
+    ts(T.bi[:, 1:2], T.pi[:], 4, 1, A.logical_shift_right, A.bitwise_and, ["pi"], ["bi"], grp="bi")
+    ts(T.bi[:, 2:3], T.pi[:], 3, 1, A.logical_shift_right, A.bitwise_and, ["pi"], ["bi"], grp="bi")
+    ts(T.bi[:, 3:4], T.pi[:], 1, None, A.bitwise_and, None, ["pi"], ["bi"], grp="bi")
+    ms(T.o32[:], 1.0, ["o32"])
+    cp(T.bf[:], T.bi[:], ["bi"], ["bf"])
+    ms(T.zr[:], 0.0, ["zr"])
+    ts(T.ev[:], od, -1.0, 1.0, A.mult, A.add, ["bf"], ["ev"])
+    ts(T.ub[:], T.eh[:, 7:39], 2.0, od, A.add, A.mult, ["bf", "eh", "eh0"], ["ub"])
+    ts(T.ta[:], T.i16[:], p16, None, A.mult, None, ["i16", "bf"], ["ta"])
+    ts(T.ua[:], T.eh[:, 8:40], T.ev[:], None, A.mult, None, ["ev", "eh"], ["ua"])
+    ts(T.ub[:, 16:17], T.ub[:, 16:17], od, None, A.add, None, ["ub", "bf"], ["ub"])
+    ts(T.tb[:], T.ta[:], 1, None, A.logical_shift_right, None, ["ta"], ["tb"])
+    ts(T.tri[:], T.i16[:], p16, 1024.0, A.is_ge, A.mult, ["bf", "i16"], ["tri"])
+    ts(T.diag[:], T.i16[:], p16, None, A.is_equal, None, ["bf", "i16"], ["diag"])
+    ts(T.eq[:, 16:17], T.pi[:], p16, None, A.subtract, None, ["pi", "bf"], ["g16"])
+    for q in range(N):
+        tt(T.utab[:, 32 * q:32 * q + 32], T.ua[:], T.ub[:], A.add, ["ua", "ub"], ["utab"], grp="utab")
+    tt(T.tab2[:], T.tb[:], T.tab8[:], A.subtract, ["tb", "tab8"], ["tab2"])
+    op("t", lambda q: q.matmul(T.ps[:, 0:12], T.one[0:1, :], T.t2[0:1, :], True, False), ["one", "t2"], [], inc=0)
+
+    cp(T.wu[:, 0:1], T.wt[:], ["wt"], ["wu"])
+    ts(T.qk[:], T.wt[:], -15.5, RND, A.add, A.add, ["wt"], ["qk"])
+    tt(T.z[:], T.tabq[:].indirect(T.wu[:, 0:1]), T.tri[:], A.add, ["tabq", "wu", "tri"], ["z"])
+    ts(T.q32[:], T.qk[:], -RND, None, A.add, None, ["qk"], ["q32"])
+    tt(T.ud[:], T.utab[:].indirect(T.wu[:, 0:1]), T.diag[:], A.mult, ["utab", "wu", "diag"], ["ud"])
+    ts(T.eq[:, 0:16], T.z[:], T.q32[:], None, A.is_equal, None, ["z", "q32"], ["eq"])
+    red(T.u[:], T.ud[:], ["ud"], ["u"])
+    red(T.rk[:], T.eq[:], ["eq", "g16"], ["rk"])
+    ts(T.rh[:], T.qc[:], T.q32[:], T.u[:], A.is_equal, A.mult, ["qc", "q32", "u"], ["rh"])
+    ts(T.lh[:], T.isl[:], T.rk[:], 8.0, A.is_equal, A.mult, ["isl", "rk"], ["lh"])
+    op("t", lambda q: q.matmul(T.ps[:, 0:12], T.lh[:], T.rh[:], False, True), ["lh", "rh"], ["ps"])
+    cp(T.wdu[:, 0:4:2], T.wdi[:], ["wdi"], ["wdu"])
+    ms(T.hf[:], 0.5, ["hf"])
+    ts(T.msg[:, :, 0:3], T.ps[:, 0:12], kk, None, A.add, None, ["ps", "bf"], ["msgl"])
+    nq = sum(send(T.msg[:, p, 0:3], T.req[:, me, 0:3], "rq", "lq", p, ["msgl"]) for p in ask)
+    op("g", lambda q: q.sem_inc(T.sem.gq, 1), [], [], inc=0)
+    iota(T.c16[:], [[0, 2], [1, 8]], 0, 0, ["c16"])
+    iota(T.ab8[:], [[8, 2], [0, 8]], 0, 0, ["ab8"])
+    iota(T.ab40[:], [[ZB, 2], [0, 8]], 0, 0, ["ab40"])
+    dma("s", T.wall[:, 2 * me:2 * me + 2], T.wd[:], [], ["wall"], grp="wall")
+    for p in tell:
+        dma("s", T.wall[:, 2 * p:2 * p + 2], T.win4[p], [], ["wall"], grp="wall", ext=[("wq", sum(arrivals(r) for r in tell))])
+    dma("s", T.dc[:, 0:D0], T.dic[:, 0:D0], [], ["dc0"], ext=[("gq", 1)])
+
+    for h in range(2):
+        act(T.w8[:, 16 * h:16 * h + 16], T.tab8[:].indirect(T.wdu[:, 2 * h:2 * h + 1]), ["tab8", "wdu"], ["w8"], grp="w8")
+    for h in range(2):
+        act(T.dx[:, 16 * h:16 * h + 16], T.tab2[:].indirect(T.wdu[:, 2 * h:2 * h + 1]), ["tab2", "wdu"], ["dx"], grp="dx",
+            f=IDENT, bias=-float(HB * h))
+    op("v", lambda q: q.tensor_tensor_scan(T.pw[:], T.hf[:], T.zr[:], 2.0, A.mult, A.add), ["hf", "zr"], ["pw"])
+    op("v", lambda q: q.tensor_tensor_scan(T.inc[:], T.o32[:], T.w8[:], 0.0, A.mult, A.add), ["o32", "w8"], ["inc"])
+    ms(T.pt[:], 0.0, ["pt"])
+    tt(T.xs[:], T.dx[:], T.inc[:], A.add, ["dx", "inc"], ["xs"])
+    ts(T.pev[:], pod, -1.0, 1.0, A.mult, A.add, ["bf"], ["pev"])
+    cp(T.o1[:], T.xs[:], ["xs"], ["o1"])
+    ts(T.pt[:, 0:ZB], T.pw[:], 65536.0, 1.0, A.mult, A.max, ["pw", "pt"], ["pt1"], grp="pt1")
+    ts(T.pt[:, ZB + 17:2 * ZB], T.pw[:, 17:ZB], 4294967296.0, None, A.mult, None, ["pw", "pt"], ["pt1"], grp="pt1")
+    cp(T.pt[:, 2 * ZB:2 * ZB + 16], T.pw[:, 0:16], ["pw", "pt"], ["pt1"], grp="pt1")
+    act(T.pa[:], T.pt[:, 0:ZZ], ["pt1", "pev"], ["pa"], f=IDENT, scale=T.pev[:])
+    act(T.pb[:], T.pt[:, 8:ZZ + 8], ["pt1", "bf"], ["pb"], f=IDENT, scale=pod)
+    cp(T.gw[:, 512:528], T.win[:].indirect(T.o1[:, 0:1]), ["win", "wtail", "o1"], ["gw"], grp="gw")
+    cp(T.gw[:, 0:512], T.win[:].indirect(T.o1[:]), ["win", "wtail", "o1"], ["gw"], grp="gw")
+    op("v", lambda q: q.transpose(T.tw[:, 0:512], T.gw[:, 0:512]), ["gw"], ["tw"], grp="tw")
+    op("v", lambda q: q.transpose(T.tw[:, 512:1024], T.gw[:, 16:528]), ["gw"], ["tw"], grp="tw")
+
+    na = 0
+    for p in tell:
+        cp(T.rsp[:, p, :], T.tw[:].indirect(T.req[:, p, 0:3]), ["tw"], ["rsp%d" % p], ext=[("rq%d" % p, arrivals(p))])
+        na += send(T.rsp[:, p, :], T.ans[:, me, :], "an", "la", p, ["rsp%d" % p])
+        if p == tell[0]:
+            ms(T.rf[:, 192:200], 0.0, ["rfp"])
+            ts(T.sq[:], T.q32[:], 1.5, T.rk[:], A.mult, A.add, ["q32", "rk"], ["sq"])
+            cp(T.rf[:, 48 * me:48 * me + 48], T.tw[:].indirect(T.msg[:, me, 0:3]), ["tw", "msgl"], ["rf"], grp="rf")
+        if p == tell[1]:
+            tt(T.pt[:, ZZ:2 * ZZ], T.pa[:], T.pb[:], A.add, ["pa", "pb", "pt1"], ["pt2"])
+            ts(T.ab8s[:], T.ab8[:], T.sq[:], T.eq[:, 16:17], A.add, A.subtract, ["ab8", "sq", "g16"], ["ab8s"])
+    op("g", lambda q: q.sem_inc(T.sem.ga, 1), [], [], inc=0)
+    dma("s", T.dc[:, D0:4096], T.dic[:, D0:4096], [], ["dc1"], ext=[("ga", 1)])
+
+    cp(T.walu[:], T.wall[:], ["wall"], ["walu"])
+    act(T.wrep[:], T.i16[:].indirect(T.walu[:]), ["i16", "walu"], ["wrep"])
+    tt(T.wdg[:], T.wrep[:].indirect(T.wu[:, 0:1]), T.diag[:], A.mult, ["wrep", "wu", "diag"], ["wdg"])
+    red(T.wi[:], T.wdg[:], ["wdg"], ["wi"])
+    cp(T.wii[:], T.wi[:], ["wi"], ["wii"])
+    ts(T.cw[:], T.c16[:], T.wi[:], None, A.mult, None, ["c16", "wi"], ["cw"])
+    ts(T.x3[:], T.zr[:, 0:8], T.wi[:], float(2 * ZB + 16), A.subtract, A.add, ["zr", "wi"], ["x3"])
+    ts(T.woi[:], T.wii[:], 1, None, A.bitwise_and, None, ["wii"], ["woi"])
+    ts(T.po[:], T.cw[:], 15, None, A.bitwise_and, None, ["cw"], ["po"])
+    ts(T.fo[:], T.cw[:], 1, 0x78, A.logical_shift_right, A.bitwise_and, ["cw"], ["fo"])
+    act(T.m2[:, 128:256], T.pt[:, 0:2 * ZZ].indirect(T.x3[:]), ["pt1", "pt2", "x3"], ["m2b"])
+    ts(T.zo[:], T.woi[:], float(ZZ), None, A.mult, None, ["woi"], ["zo"])
+    tt(T.j1[:], T.po[:], T.ab40[:], A.add, ["po", "ab40"], ["j1"])
+    tt(T.j2[:], T.fo[:], T.ab8s[:], A.add, ["fo", "ab8s"], ["j2"])
+    ts(T.x1[:], T.j1[:], T.zo[:], T.wi[:], A.add, A.add, ["j1", "zo", "wi"], ["x1"])
+    ts(T.x2[:], T.j1[:, 0:8], T.zo[:], float(2 * ZB), A.add, A.add, ["j1", "zo"], ["x2"])
+    act(T.m1[:], T.pt[:, 0:2 * ZZ].indirect(T.x1[:]), ["pt1", "pt2", "x1"], ["m1"])
+    cp(T.o2[:], T.j2[:], ["j2"], ["o2"])
+    tt(T.m2[:, 0:128], T.pt[:, 0:2 * ZZ].indirect(T.x2[:]), T.m2[:, 128:256], A.min, ["pt1", "pt2", "x2", "m2b"], ["m2a"])
+    act(T.pm[:, 0:256], T.m2[:], ["m2a", "m2b"], ["pm"])
+
+    for p in ask:
+        cp(T.rf[:, 48 * p:48 * p + 48], T.ans[:, p, :], [], ["rf"], grp="rf", ext=[("an%d" % p, arrivals(p))])
+    tt(T.ya[:], T.rf[:].indirect(T.o2[:]), T.m1[:], A.mult, ["rf", "rfp", "o2", "m1"], ["ya"])
+    ts(T.yb[:], T.ya[:], 0xFFF0, None, A.bitwise_and, None, ["ya"], ["yb"])
+    tt(T.pc[:, 0:128], T.yb[:, 0:128], T.pm[:, 0:128], A.mult, ["yb", "pm"], ["yc"], grp="yc")
+    tt(T.yc[:], T.yb[:, 128:256], T.pm[:, 128:256], A.mult, ["yb", "pm"], ["yc"], grp="yc")
+    tt(T.yd[:], T.yc[:], T.pc[:, 0:128], A.add, ["yc"], ["yd"])
+    ts(T.cu[:], T.yd[:], -0.5 + 2.0 ** -12, None, A.add, None, ["yd"], ["cu"])
+    for h in range(2):
+        for c in range(8):
+            out = T.ob[:, 1024 * h + c:1024 * h + 1024:8]
+            src = T.dc[:].indirect(T.cu[:, 16 * c + 8 * h:16 * c + 8 * h + 8])
+            if c % 2 == 0:
+                cp(out, src, ["dc0", "dc1", "cu"], ["ov%d" % h], grp="ov%d" % h)
+            else:
+                act(out, src, ["dc0", "dc1", "cu"], ["oa%d" % h], grp="oa%d" % h)
+        dma("s", T.y[:, 1024 * h:1024 * h + 1024], T.ob[:, 1024 * h:1024 * h + 1024], ["ov%d" % h, "oa%d" % h], ["y"], grp="y")
+    op("s", lambda q: None, ["y"], [], inc=0, ext=[("la", na), ("lq", nq), ("lw", nw)])
+
+    emit(ops, {"g": g, "v": g.vector, "a": g.scalar, "s": g.sync, "t": g.tensor}, T)

@@ -1,59 +1,26 @@
 from concourse.bass import DstId, RemoteDMATransfer
-from concourse.mybir import AluOpType, AxisListType, ActivationFunctionType
+from concourse.mybir import AluOpType as A, AxisListType, ActivationFunctionType as AF
 
-N = 4
-S = 2176
-HB = 512
-WN = S - HB
-H0 = 1536
-ZB = 40
-ZZ = 3 * ZB
+N, S, HB, H0, ZB = 4, 2176, 512, 1536, 40
+WN, ZZ = S - HB, 3 * ZB
 RND = 402653184.0
-D0 = 1536
 
-F, I, U, BF = "float32", "int32", "uint16", "bfloat16"
-SCRATCH = {
-    "win": ("sbuf", [128, WN], I), "dc": ("sbuf", [128, 4096], BF), "ob": ("sbuf", [128, 2048], BF),
-    "wt": ("sbuf", [128, 1], I), "wdi": ("sbuf", [128, 2], I), "wdu": ("sbuf", [128, 4], U),
-    "wout": ("dram", [128, 2], I), "win4": ("dram", [N, 128, 2], I), "wall": ("sbuf", [128, 2 * N], I), "walu": ("sbuf", [128, 2 * N], U),
-    "pi": ("sbuf", [128, 1], I), "bi": ("sbuf", [128, 4], I), "bf": ("sbuf", [128, 4], F),
-    "ev": ("sbuf", [128, 1], F), "pev": ("sbuf", [128, 1], F),
-    "i16": ("sbuf", [128, 16], F), "tabq": ("sbuf", [128, 128], F), "isl": ("sbuf", [128, 128], F),
-    "eh": ("sbuf", [128, 40], F), "ua": ("sbuf", [128, 32], F), "ub": ("sbuf", [128, 32], F), "utab": ("sbuf", [128, 128], F),
-    "qc": ("sbuf", [128, 12], F), "t2": ("sbuf", [128, 12], BF), "one": ("sbuf", [128, 128], BF),
-    "tri": ("sbuf", [128, 16], F), "diag": ("sbuf", [128, 16], F),
-    "wu": ("sbuf", [128, 2], U), "qk": ("sbuf", [128, 1], F), "q32": ("sbuf", [128, 1], F),
-    "z": ("sbuf", [128, 16], F), "eq": ("sbuf", [128, 17], F), "rk": ("sbuf", [128, 1], F),
-    "ud": ("sbuf", [128, 16], F), "u": ("sbuf", [128, 1], F),
-    "lh": ("sbuf", [128, 128], BF), "rh": ("sbuf", [128, 12], BF),
-    "msg": ("sbuf", [128, N, 4], U), "req": ("sbuf", [128, N, 4], U),
-    "tab8": ("sbuf", [128, 16], F), "o32": ("sbuf", [128, 32], F),
-    "ta": ("sbuf", [128, 16], I), "tb": ("sbuf", [128, 16], I), "tab2": ("sbuf", [128, 16], F),
-    "w8": ("sbuf", [128, 32], F), "dx": ("sbuf", [128, 32], F), "inc": ("sbuf", [128, 32], F), "xs": ("sbuf", [128, 32], F),
-    "o1": ("sbuf", [128, 32], U),
-    "gw": ("sbuf", [128, 528], F), "tw": ("sbuf", [128, 1024], F),
-    "rsp": ("sbuf", [128, N, 48], U), "ans": ("sbuf", [128, N, 48], U), "rf": ("sbuf", [128, 200], F),
-    "hf": ("sbuf", [128, ZB], F), "zr": ("sbuf", [128, ZB], F), "pw": ("sbuf", [128, ZB], F),
-    "pt": ("sbuf", [128, 2 * ZZ + 8], F), "pa": ("sbuf", [128, ZZ], F), "pb": ("sbuf", [128, ZZ], F),
-    "c16": ("sbuf", [128, 16], F), "ab8": ("sbuf", [128, 16], F), "ab40": ("sbuf", [128, 16], F),
-    "wrep": ("sbuf", [128, 128], F), "wdg": ("sbuf", [128, 16], F), "wi": ("sbuf", [128, 1], F),
-    "wii": ("sbuf", [128, 1], I), "woi": ("sbuf", [128, 1], I), "zo": ("sbuf", [128, 1], F), "sq": ("sbuf", [128, 1], F),
-    "cw": ("sbuf", [128, 16], I), "po": ("sbuf", [128, 16], I), "fo": ("sbuf", [128, 16], I),
-    "j1": ("sbuf", [128, 16], F), "j2": ("sbuf", [128, 16], F), "ab8s": ("sbuf", [128, 16], F),
-    "x1": ("sbuf", [128, 16], U), "x2": ("sbuf", [128, 8], U), "x3": ("sbuf", [128, 8], U), "o2": ("sbuf", [128, 16], U),
-    "m1": ("sbuf", [128, 256], F), "m2": ("sbuf", [128, 256], F),
-    "ya": ("sbuf", [128, 256], I), "yb": ("sbuf", [128, 256], I), "yc": ("sbuf", [128, 128], F), "yd": ("sbuf", [128, 128], F),
-    "cu": ("sbuf", [128, 128], U),
-    "ps": ("psum", [128, 512], F), "pm": ("psum", [128, 512], F), "pc": ("psum", [128, 512], F),
-}
-NS = 128
-SEMAPHORES = (["s%d" % k for k in range(NS)] + ["rq%d" % k for k in range(N)] + ["an%d" % k for k in range(N)]
-              + ["wq", "lw", "lq", "la", "gq", "ga"])
-
-A = AluOpType
-X = AxisListType.X
-COPY = ActivationFunctionType.Copy
-IDENT = ActivationFunctionType.Identity
+SCRATCH = {"wout": ("dram", [128, 2], "int32"), "win4": ("dram", [N, 128, 2], "int32"),
+           "msg": ("sbuf", [128, N, 4], "uint16"), "req": ("sbuf", [128, N, 4], "uint16"),
+           "rsp": ("sbuf", [128, N, 48], "uint16"), "ans": ("sbuf", [128, N, 48], "uint16")}
+for _t, _s in (("int32", "win:1664 wt:1 wdi:2 wall:8 pi:1 bi:4 ta:16 tb:16 cw:8 po:8 fo:8 ya:256 yb:256"),
+               ("uint16", "wdu:4 walu:8 wu:2 o1:34 x1:16 x2:8 x3:8 o2:16 cu:128"),
+               ("bfloat16", "dc:4096 ob:2048 t2:12 one:128 lh:128 rh:12"),
+               ("float32", "bf:4 ev:1 i16:16 tabq:128 isl:128 eh:40 ua:32 ub:32 utab:128 qc:12 tri:16 diag:16 qk:1 q32:1 "
+                           "z:16 eq:17 rk:1 ud:16 u:1 tab8:16 o32:32 tab2:16 w8:32 dx:32 inc:32 xs:33 gw:528 tw:1024 rf:200 "
+                           "pw:64 pt:240 k16:8 tz:16 wrep:128 zrep:128 wdg:16 zdg:16 wi:1 zw:1 sq:1 sr:1 ng:1 "
+                           "m1:256 m2:256 yc:128 yd:128")):
+    for _e in _s.split():
+        SCRATCH[_e.split(":")[0]] = ("sbuf", [128, int(_e.split(":")[1])], _t)
+for _e in ("ps", "pm", "pc"):
+    SCRATCH[_e] = ("psum", [128, 512], "float32")
+SEMAPHORES = (["s%d" % k for k in range(128)] + ["rq%d" % k for k in range(N)] + ["an%d" % k for k in range(N)]
+              + ["wq", "lw", "lq", "la"])
 
 
 def emit(ops, queues, T):
@@ -113,7 +80,7 @@ def rank_program(g, core, T, topo):
     ops = []
 
     def op(q, f, r, w, grp=None, inc=1, ext=()):
-        ops.append({"q": q, "f": f, "r": list(r), "w": list(w), "grp": grp, "inc": inc, "ext": list(ext)})
+        ops.append({"q": q, "f": f, "r": r.split(), "w": w.split(), "grp": grp, "inc": inc, "ext": list(ext)})
 
     def ts(out, in0, s1, s2, o0, o1, r, w, **kw):
         if o1 is None:
@@ -127,179 +94,176 @@ def rank_program(g, core, T, topo):
     def cp(out, a, r, w, **kw):
         op("v", lambda q: q.tensor_copy(out, a), r, w, **kw)
 
-    def ms(out, c, w, **kw):
-        op("v", lambda q: q.memset(out, c), [], w, **kw)
+    def ms(out, c, w):
+        op("v", lambda q: q.memset(out, c), "", w)
 
     def red(out, a, r, w):
-        op("v", lambda q: q.tensor_reduce(out, a, X, A.add), r, w)
+        op("v", lambda q: q.tensor_reduce(out, a, AxisListType.X, A.add), r, w)
 
-    def act(out, a, r, w, f=COPY, grp=None, **kw):
-        op("a", lambda q: q.activation(out, a, f, **kw), r, w, grp=grp)
+    def act(out, a, r, w, grp=None, **kw):
+        op("a", lambda q: q.activation(out, a, AF.Identity if kw else AF.Copy, **kw), r, w, grp=grp)
 
     def dma(qn, out, a, r, w, **kw):
         op(qn, lambda q: q.dma_start(out, a), r, w, inc=16, **kw)
 
-    def iota(out, pat, base, cm, w, flt=True):
-        if flt:
-            op("g", lambda q: q.iota(out, pat, base, cm, allow_small_or_imprecise_dtypes=True), [], w)
-        else:
-            op("g", lambda q: q.iota(out, pat, base, cm), [], w)
+    def iota(out, pat, w):
+        op("g", lambda q: q.iota(out, pat, 0, 0, allow_small_or_imprecise_dtypes=True), "", w)
 
     def send(src, dst, sem, local, p, r):
         rid, pid, _ = topo.addr(T.cores[p])
         op("g", lambda q: q.remote_dma(dst, src, T.sem["%s%d" % (sem, me)], T.sem[local], pid, rid,
-                                       topo.mask(core, T.cores[p])), r, [], inc=0)
+                                       topo.mask(core, T.cores[p])), r, "", inc=0)
         return len(topo.engines(core, T.cores[p]))
 
     def arrivals(p):
         return len(topo.engines(T.cores[p], core))
 
-    p16, od, kk, pod = T.bf[:, 0:1], T.bf[:, 1:2], T.bf[:, 2:3], T.bf[:, 3:4]
+    p16, od, kk = T.bf[:, 0:1], T.bf[:, 1:2], T.bf[:, 2:3]
+    SHR, AND = A.logical_shift_right, A.bitwise_and
 
-    ms(T.win[:, H0:WN], 0, ["wtail"])
-    dma("a", T.wout[:], T.wd[:], [], ["wout"])
-    dma("s", T.wt[:], T.want[:], [], ["wt"])
-    dma("a", T.wdi[:], T.wd[:], [], ["wdi"])
+    ms(T.win[:, H0:WN], 0, "wtail")
+    dma("a", T.wdi[:], T.wd[:], "", "wdi")
+    dma("s", T.wt[:], T.want[:], "", "wt")
+    dma("a", T.wout[:], T.wd[:], "", "wout")
     for k in range(8):
-        dma("sa"[k % 2], T.win[k::16, 0:H0], T.strm[:, k:k + H0], [], ["win"], grp="win")
+        dma("sa"[k % 2], T.win[k::16, 0:H0], T.strm[:, k:k + H0], "", "win", grp="win")
     for k in range(8):
-        dma("as"[k < 5], T.win[8 + k::16, 0:WN - k], T.strm[:, HB + k:S], ["wtail"], ["win"], grp="win")
+        dma("as"[k < 5], T.win[8 + k::16, 0:WN - k], T.strm[:, HB + k:S], "wtail", "win", grp="win")
+    dma("s", T.dc[:], T.dic[:], "", "dc0")
 
-    iota(T.pi[:], [[0, 1]], 0, 1, ["pi"], flt=False)
-    iota(T.i16[:], [[1, 16]], 0, 0, ["i16"])
-    iota(T.eh[:, 8:40], [[33, 2], [4, 8], [64, 2]], 0, 0, ["eh"])
-    iota(T.tabq[:], [[32, 4], [0, 32]], 0, 0, ["tabq"])
-    iota(T.qc[:], [[32, 4], [0, 3]], 0, 0, ["qc"])
-    iota(T.isl[:], [[16, 8], [0, 2], [1, 8]], 0, 0, ["isl"])
-    iota(T.t2[0:1, :], [[0, 4], [2, 3]], 0, 0, ["t2"])
+    op("g", lambda q: q.iota(T.pi[:], [[0, 1]], 0, 1), "", "pi")
+    iota(T.i16[:], [[1, 16]], "i16")
+    iota(T.eh[:, 8:40], [[33, 2], [4, 8], [64, 2]], "eh")
+    iota(T.tabq[:], [[32, 4], [0, 32]], "tabq")
+    iota(T.qc[:], [[32, 4], [0, 3]], "qc")
+    iota(T.isl[:], [[16, 8], [0, 2], [1, 8]], "isl")
+    iota(T.t2[0:1, :], [[0, 4], [2, 3]], "t2")
 
     far = [topo.addr(T.cores[p]) for p in ask]
     wtr = RemoteDMATransfer(dst_ids=[DstId(rid=a[0], pnc=a[1]) for a in far], dma_engine_mask=topo.mask(core, T.cores[ask[0]]),
                             remote_sem=T.sem.wq, srcs=[T.wout[:]], dsts=[T.win4[me] for _ in far])
-    op("g", lambda q: q.remote_dma_fused([wtr], local_sem=T.sem.lw), ["wout"], [], inc=0)
+    op("g", lambda q: q.remote_dma_fused([wtr], local_sem=T.sem.lw), "wout", "", inc=0)
     nw = len(topo.engines(core, T.cores[ask[0]]))
 
-    act(T.tab8[:], T.i16[:], ["i16"], ["tab8"], f=IDENT, scale=8.0)
-    ms(T.one[0:1, :], 1.0, ["one"])
-    ms(T.eh[:, 7:8], 124.0, ["eh0"])
-    ts(T.bi[:, 0:1], T.pi[:], 15, None, A.bitwise_and, None, ["pi"], ["bi"], grp="bi")
-    ts(T.bi[:, 1:2], T.pi[:], 4, 1, A.logical_shift_right, A.bitwise_and, ["pi"], ["bi"], grp="bi")
-    ts(T.bi[:, 2:3], T.pi[:], 3, 1, A.logical_shift_right, A.bitwise_and, ["pi"], ["bi"], grp="bi")
-    ts(T.bi[:, 3:4], T.pi[:], 1, None, A.bitwise_and, None, ["pi"], ["bi"], grp="bi")
-    ms(T.o32[:], 1.0, ["o32"])
-    cp(T.bf[:], T.bi[:], ["bi"], ["bf"])
-    ms(T.zr[:], 0.0, ["zr"])
-    ts(T.ev[:], od, -1.0, 1.0, A.mult, A.add, ["bf"], ["ev"])
-    ts(T.ub[:], T.eh[:, 7:39], 2.0, od, A.add, A.mult, ["bf", "eh", "eh0"], ["ub"])
-    ts(T.ta[:], T.i16[:], p16, None, A.mult, None, ["i16", "bf"], ["ta"])
-    ts(T.ua[:], T.eh[:, 8:40], T.ev[:], None, A.mult, None, ["ev", "eh"], ["ua"])
-    ts(T.ub[:, 16:17], T.ub[:, 16:17], od, None, A.add, None, ["ub", "bf"], ["ub"])
-    ts(T.tb[:], T.ta[:], 1, None, A.logical_shift_right, None, ["ta"], ["tb"])
-    ts(T.tri[:], T.i16[:], p16, 1024.0, A.is_ge, A.mult, ["bf", "i16"], ["tri"])
-    ts(T.diag[:], T.i16[:], p16, None, A.is_equal, None, ["bf", "i16"], ["diag"])
-    ts(T.eq[:, 16:17], T.pi[:], p16, None, A.subtract, None, ["pi", "bf"], ["g16"])
+    act(T.tab8[:], T.i16[:], "i16", "tab8", scale=8.0)
+    act(T.o32[:], T.eh[:, 8:40], "eh", "o32", scale=0.0, bias=1.0)
+    act(T.one[0:1, :], T.tabq[0:1, :], "tabq", "one", scale=0.0, bias=1.0)
+    ms(T.eh[:, 7:8], 124.0, "eh0")
+    ts(T.bi[:, 0:1], T.pi[:], 15, None, AND, None, "pi", "bi", grp="bi")
+    ts(T.bi[:, 1:2], T.pi[:], 4, 1, SHR, AND, "pi", "bi", grp="bi")
+    ts(T.bi[:, 2:3], T.pi[:], 3, 1, SHR, AND, "pi", "bi", grp="bi")
+    cp(T.bf[:, 0:3], T.bi[:, 0:3], "bi", "bf")
+    ts(T.ta[:], T.i16[:], p16, None, A.mult, None, "i16 bf", "ta")
+    ts(T.ev[:], od, -1.0, 1.0, A.mult, A.add, "bf", "ev")
+    ts(T.ub[:], T.eh[:, 7:39], 2.0, od, A.add, A.mult, "bf eh eh0", "ub")
+    ts(T.tb[:], T.ta[:], 1, None, SHR, None, "ta", "tb")
+    ts(T.ua[:], T.eh[:, 8:40], T.ev[:], None, A.mult, None, "ev eh", "ua")
+    ts(T.ub[:, 16:17], T.ub[:, 16:17], od, None, A.add, None, "ub bf", "ub")
+    ts(T.tri[:], T.i16[:], p16, 1024.0, A.is_ge, A.mult, "bf i16", "tri")
+    ts(T.diag[:], T.i16[:], p16, None, A.is_equal, None, "bf i16", "diag")
+    ts(T.eq[:, 16:17], T.pi[:], p16, None, A.subtract, None, "pi bf", "g16")
     for q in range(N):
-        tt(T.utab[:, 32 * q:32 * q + 32], T.ua[:], T.ub[:], A.add, ["ua", "ub"], ["utab"], grp="utab")
-    tt(T.tab2[:], T.tb[:], T.tab8[:], A.subtract, ["tb", "tab8"], ["tab2"])
-    op("t", lambda q: q.matmul(T.ps[:, 0:12], T.one[0:1, :], T.t2[0:1, :], True, False), ["one", "t2"], [], inc=0)
+        tt(T.utab[:, 32 * q:32 * q + 32], T.ua[:], T.ub[:], A.add, "ua ub", "utab", grp="utab")
+    tt(T.tab2[:], T.tb[:], T.tab8[:], A.subtract, "tb tab8", "tab2")
+    op("t", lambda q: q.matmul(T.ps[:, 0:12], T.one[0:1, :], T.t2[0:1, :], True, False), "one t2", "", inc=0)
 
-    cp(T.wu[:, 0:1], T.wt[:], ["wt"], ["wu"])
-    ts(T.qk[:], T.wt[:], -15.5, RND, A.add, A.add, ["wt"], ["qk"])
-    tt(T.z[:], T.tabq[:].indirect(T.wu[:, 0:1]), T.tri[:], A.add, ["tabq", "wu", "tri"], ["z"])
-    ts(T.q32[:], T.qk[:], -RND, None, A.add, None, ["qk"], ["q32"])
-    tt(T.ud[:], T.utab[:].indirect(T.wu[:, 0:1]), T.diag[:], A.mult, ["utab", "wu", "diag"], ["ud"])
-    ts(T.eq[:, 0:16], T.z[:], T.q32[:], None, A.is_equal, None, ["z", "q32"], ["eq"])
-    red(T.u[:], T.ud[:], ["ud"], ["u"])
-    red(T.rk[:], T.eq[:], ["eq", "g16"], ["rk"])
-    ts(T.rh[:], T.qc[:], T.q32[:], T.u[:], A.is_equal, A.mult, ["qc", "q32", "u"], ["rh"])
-    ts(T.lh[:], T.isl[:], T.rk[:], 8.0, A.is_equal, A.mult, ["isl", "rk"], ["lh"])
-    op("t", lambda q: q.matmul(T.ps[:, 0:12], T.lh[:], T.rh[:], False, True), ["lh", "rh"], ["ps"])
-    cp(T.wdu[:, 0:4:2], T.wdi[:], ["wdi"], ["wdu"])
-    ms(T.hf[:], 0.5, ["hf"])
-    ts(T.msg[:, :, 0:3], T.ps[:, 0:12], kk, None, A.add, None, ["ps", "bf"], ["msgl"])
-    nq = sum(send(T.msg[:, p, 0:3], T.req[:, me, 0:3], "rq", "lq", p, ["msgl"]) for p in ask)
-    op("g", lambda q: q.sem_inc(T.sem.gq, 1), [], [], inc=0)
-    iota(T.c16[:], [[0, 2], [1, 8]], 0, 0, ["c16"])
-    iota(T.ab8[:], [[8, 2], [0, 8]], 0, 0, ["ab8"])
-    iota(T.ab40[:], [[ZB, 2], [0, 8]], 0, 0, ["ab40"])
-    dma("s", T.wall[:, 2 * me:2 * me + 2], T.wd[:], [], ["wall"], grp="wall")
+    wu = T.wu[:, 0:1]
+    cp(T.wdu[:, 0:4:2], T.wdi[:], "wdi", "wdu")
+    for h in range(2):
+        act(T.w8[:, 16 * h:16 * h + 16], T.tab8[:].indirect(T.wdu[:, 2 * h:2 * h + 1]), "tab8 wdu", "w8", grp="w8")
+    for h in range(2):
+        act(T.dx[:, 16 * h:16 * h + 16], T.tab2[:].indirect(T.wdu[:, 2 * h:2 * h + 1]), "tab2 wdu", "dx", grp="dx",
+            bias=-float(HB * h))
+    act(T.xs[:, 32:33], T.dx[:, 0:1], "dx w8", "xs0", bias=T.w8[:, 0:1])
+    cp(wu, T.wt[:], "wt", "wu")
+    ts(T.qk[:], T.wt[:], -15.5, RND, A.add, A.add, "wt", "qk")
+    tt(T.z[:], T.tabq[:].indirect(wu), T.tri[:], A.add, "tabq wu tri", "z")
+    ts(T.q32[:], T.qk[:], -RND, None, A.add, None, "qk", "q32")
+    tt(T.ud[:], T.utab[:].indirect(wu), T.diag[:], A.mult, "utab wu diag", "ud")
+    ts(T.eq[:, 0:16], T.z[:], T.q32[:], None, A.is_equal, None, "z q32", "eq")
+    op("v", lambda q: q.tensor_tensor_scan(T.inc[:], T.o32[:], T.w8[:], 0.0, A.mult, A.add), "o32 w8", "inc")
+    red(T.rk[:], T.eq[:], "eq g16", "rk")
+    red(T.u[:], T.ud[:], "ud", "u")
+    ts(T.lh[:], T.isl[:], T.rk[:], 8.0, A.is_equal, A.mult, "isl rk", "lh")
+    ts(T.rh[:], T.qc[:], T.q32[:], T.u[:], A.is_equal, A.mult, "qc q32 u", "rh")
+    op("t", lambda q: q.matmul(T.ps[:, 0:12], T.lh[:], T.rh[:], False, True), "lh rh", "ps")
+    tt(T.xs[:, 0:32], T.dx[:], T.inc[:], A.add, "dx inc", "xs")
+    cp(T.o1[:, 0:33], T.xs[:], "xs xs0", "o1")
+    ts(T.msg[:, :, 0:3], T.ps[:, 0:12], kk, None, A.add, None, "ps bf", "msgl")
+    nq = sum(send(T.msg[:, p, 0:3], T.req[:, me, 0:3], "rq", "lq", p, "msgl") for p in ask)
+    iota(T.tz[:], [[2, 8], [ZZ + 1, 2]], "tz")
+
+    cp(T.gw[:], T.win[:].indirect(T.o1[:, 0:33]), "win wtail o1", "gw")
+    op("v", lambda q: q.transpose(T.tw[:, 0:512], T.gw[:, 0:512]), "gw", "tw", grp="tw")
+    op("v", lambda q: q.transpose(T.tw[:, 512:1024], T.gw[:, 16:528]), "gw", "tw", grp="tw")
+
+    act(T.pw[:, 0:1], T.i16[:, 0:1], "i16", "pw", bias=1.0)
+    act(T.ng[:], T.eq[:, 16:17], "g16", "ng", scale=-1.0)
+    for j in range(6):
+        n = 1 << j
+        act(T.pw[:, n:2 * n], T.pw[:, 0:n], "pw", "pw", scale=2.0 ** -n)
+        if j == 0:
+            act(T.sq[:], T.q32[:], "q32 rk", "sq", scale=1.5, bias=T.rk[:])
+        if j == 1:
+            act(T.k16[:], T.i16[:, 0:8], "i16", "k16", scale=0.0, bias=16.0)
+        if j == 2:
+            act(T.sr[:], T.sq[:], "sq ng", "sr", bias=T.ng[:])
+        if j == 3:
+            act(T.rf[:, 192:200], T.i16[:, 0:8], "i16", "rfp", scale=0.0)
+    for a, b, c, s, o in ((0, 16, 0, 1.0, 0.0), (16, 40, 16, 0.0, 0.0), (40, 57, 0, 65536.0, 0.0), (57, 80, 17, 0.0, 1.0),
+                          (80, 97, 0, 0.0, 0.0), (97, 120, 17, 4294967296.0, 0.0), (232, 240, 0, 0.0, 0.0)):
+        act(T.pt[:, a:b], T.pw[:, c:c + b - a], "pw", "pt1", grp="pt1", scale=s, bias=o)
+    dma("s", T.wall[:, 2 * me:2 * me + 2], T.wd[:], "", "wall", grp="wall")
     for p in tell:
-        dma("s", T.wall[:, 2 * p:2 * p + 2], T.win4[p], [], ["wall"], grp="wall", ext=[("wq", sum(arrivals(r) for r in tell))])
-    dma("s", T.dc[:, 0:D0], T.dic[:, 0:D0], [], ["dc0"], ext=[("gq", 1)])
-
-    for h in range(2):
-        act(T.w8[:, 16 * h:16 * h + 16], T.tab8[:].indirect(T.wdu[:, 2 * h:2 * h + 1]), ["tab8", "wdu"], ["w8"], grp="w8")
-    for h in range(2):
-        act(T.dx[:, 16 * h:16 * h + 16], T.tab2[:].indirect(T.wdu[:, 2 * h:2 * h + 1]), ["tab2", "wdu"], ["dx"], grp="dx",
-            f=IDENT, bias=-float(HB * h))
-    op("v", lambda q: q.tensor_tensor_scan(T.pw[:], T.hf[:], T.zr[:], 2.0, A.mult, A.add), ["hf", "zr"], ["pw"])
-    op("v", lambda q: q.tensor_tensor_scan(T.inc[:], T.o32[:], T.w8[:], 0.0, A.mult, A.add), ["o32", "w8"], ["inc"])
-    ms(T.pt[:], 0.0, ["pt"])
-    tt(T.xs[:], T.dx[:], T.inc[:], A.add, ["dx", "inc"], ["xs"])
-    ts(T.pev[:], pod, -1.0, 1.0, A.mult, A.add, ["bf"], ["pev"])
-    cp(T.o1[:], T.xs[:], ["xs"], ["o1"])
-    ts(T.pt[:, 0:ZB], T.pw[:], 65536.0, 1.0, A.mult, A.max, ["pw", "pt"], ["pt1"], grp="pt1")
-    ts(T.pt[:, ZB + 17:2 * ZB], T.pw[:, 17:ZB], 4294967296.0, None, A.mult, None, ["pw", "pt"], ["pt1"], grp="pt1")
-    cp(T.pt[:, 2 * ZB:2 * ZB + 16], T.pw[:, 0:16], ["pw", "pt"], ["pt1"], grp="pt1")
-    act(T.pa[:], T.pt[:, 0:ZZ], ["pt1", "pev"], ["pa"], f=IDENT, scale=T.pev[:])
-    act(T.pb[:], T.pt[:, 8:ZZ + 8], ["pt1", "bf"], ["pb"], f=IDENT, scale=pod)
-    cp(T.gw[:, 512:528], T.win[:].indirect(T.o1[:, 0:1]), ["win", "wtail", "o1"], ["gw"], grp="gw")
-    cp(T.gw[:, 0:512], T.win[:].indirect(T.o1[:]), ["win", "wtail", "o1"], ["gw"], grp="gw")
-    op("v", lambda q: q.transpose(T.tw[:, 0:512], T.gw[:, 0:512]), ["gw"], ["tw"], grp="tw")
-    op("v", lambda q: q.transpose(T.tw[:, 512:1024], T.gw[:, 16:528]), ["gw"], ["tw"], grp="tw")
+        dma("s", T.wall[:, 2 * p:2 * p + 2], T.win4[p], "", "wall", grp="wall", ext=[("wq", sum(arrivals(r) for r in tell))])
+    dma("a", T.pt[0::2, ZZ:2 * ZZ - 8], T.pt[0::2, 0:ZZ - 8], "pt1", "pt2", grp="pt2")
+    dma("a", T.pt[1::2, ZZ:2 * ZZ - 8], T.pt[1::2, 8:ZZ], "pt1", "pt2", grp="pt2")
 
     na = 0
     for p in tell:
-        cp(T.rsp[:, p, :], T.tw[:].indirect(T.req[:, p, 0:3]), ["tw"], ["rsp%d" % p], ext=[("rq%d" % p, arrivals(p))])
-        na += send(T.rsp[:, p, :], T.ans[:, me, :], "an", "la", p, ["rsp%d" % p])
-        if p == tell[0]:
-            ms(T.rf[:, 192:200], 0.0, ["rfp"])
-            ts(T.sq[:], T.q32[:], 1.5, T.rk[:], A.mult, A.add, ["q32", "rk"], ["sq"])
-            cp(T.rf[:, 48 * me:48 * me + 48], T.tw[:].indirect(T.msg[:, me, 0:3]), ["tw", "msgl"], ["rf"], grp="rf")
-        if p == tell[1]:
-            tt(T.pt[:, ZZ:2 * ZZ], T.pa[:], T.pb[:], A.add, ["pa", "pb", "pt1"], ["pt2"])
-            ts(T.ab8s[:], T.ab8[:], T.sq[:], T.eq[:, 16:17], A.add, A.subtract, ["ab8", "sq", "g16"], ["ab8s"])
-    op("g", lambda q: q.sem_inc(T.sem.ga, 1), [], [], inc=0)
-    dma("s", T.dc[:, D0:4096], T.dic[:, D0:4096], [], ["dc1"], ext=[("ga", 1)])
+        cp(T.rsp[:, p, :], T.tw[:].indirect(T.req[:, p, 0:3]), "tw", "rsp%d" % p, ext=[("rq%d" % p, arrivals(p))])
+        na += send(T.rsp[:, p, :], T.ans[:, me, :], "an", "la", p, "rsp%d" % p)
 
-    cp(T.walu[:], T.wall[:], ["wall"], ["walu"])
-    act(T.wrep[:], T.i16[:].indirect(T.walu[:]), ["i16", "walu"], ["wrep"])
-    tt(T.wdg[:], T.wrep[:].indirect(T.wu[:, 0:1]), T.diag[:], A.mult, ["wrep", "wu", "diag"], ["wdg"])
-    red(T.wi[:], T.wdg[:], ["wdg"], ["wi"])
-    cp(T.wii[:], T.wi[:], ["wi"], ["wii"])
-    ts(T.cw[:], T.c16[:], T.wi[:], None, A.mult, None, ["c16", "wi"], ["cw"])
-    ts(T.x3[:], T.zr[:, 0:8], T.wi[:], float(2 * ZB + 16), A.subtract, A.add, ["zr", "wi"], ["x3"])
-    ts(T.woi[:], T.wii[:], 1, None, A.bitwise_and, None, ["wii"], ["woi"])
-    ts(T.po[:], T.cw[:], 15, None, A.bitwise_and, None, ["cw"], ["po"])
-    ts(T.fo[:], T.cw[:], 1, 0x78, A.logical_shift_right, A.bitwise_and, ["cw"], ["fo"])
-    act(T.m2[:, 128:256], T.pt[:, 0:2 * ZZ].indirect(T.x3[:]), ["pt1", "pt2", "x3"], ["m2b"])
-    ts(T.zo[:], T.woi[:], float(ZZ), None, A.mult, None, ["woi"], ["zo"])
-    tt(T.j1[:], T.po[:], T.ab40[:], A.add, ["po", "ab40"], ["j1"])
-    tt(T.j2[:], T.fo[:], T.ab8s[:], A.add, ["fo", "ab8s"], ["j2"])
-    ts(T.x1[:], T.j1[:], T.zo[:], T.wi[:], A.add, A.add, ["j1", "zo", "wi"], ["x1"])
-    ts(T.x2[:], T.j1[:, 0:8], T.zo[:], float(2 * ZB), A.add, A.add, ["j1", "zo"], ["x2"])
-    act(T.m1[:], T.pt[:, 0:2 * ZZ].indirect(T.x1[:]), ["pt1", "pt2", "x1"], ["m1"])
-    cp(T.o2[:], T.j2[:], ["j2"], ["o2"])
-    tt(T.m2[:, 0:128], T.pt[:, 0:2 * ZZ].indirect(T.x2[:]), T.m2[:, 128:256], A.min, ["pt1", "pt2", "x2", "m2b"], ["m2a"])
-    act(T.pm[:, 0:256], T.m2[:], ["m2a", "m2b"], ["pm"])
+    ptw = T.pt[:]
+    cp(T.walu[:], T.wall[:], "wall", "walu")
+    act(T.wrep[:], T.i16[:].indirect(T.walu[:]), "i16 walu", "wrep")
+    act(T.zrep[:], T.tz[:].indirect(T.walu[:]), "tz walu", "zrep")
+    cp(T.rf[:, 48 * me:48 * me + 48], T.tw[:].indirect(T.msg[:, me, 0:3]), "tw msgl", "rf", grp="rf")
+    tt(T.wdg[:], T.wrep[:].indirect(wu), T.diag[:], A.mult, "wrep wu diag", "wdg")
+    red(T.wi[:], T.wdg[:], "wdg", "wi")
+    ts(T.cw[:], T.i16[:, 0:8], T.wi[:], None, A.mult, None, "i16 wi", "cw")
+    ts(T.x3[:], T.k16[:], T.wi[:], None, A.subtract, None, "k16 wi", "x3")
+    tt(T.zdg[:], T.zrep[:].indirect(wu), T.diag[:], A.mult, "zrep wu diag", "zdg")
+    ts(T.po[:], T.cw[:], 15, None, AND, None, "cw", "po")
+    red(T.zw[:], T.zdg[:], "zdg", "zw")
+    act(T.m2[:, 128:256], ptw.indirect(T.x3[:]), "pt1 pt2 x3", "m2b")
+    ts(T.fo[:], T.cw[:], 1, 0x78, SHR, AND, "cw", "fo")
+    ts(T.x1[:, 0:8], T.po[:], T.zw[:], float(ZB), A.add, A.add, "po zw", "x1", grp="x1")
+    ts(T.x1[:, 8:16], T.po[:], T.zw[:], float(2 * ZB), A.add, A.add, "po zw", "x1", grp="x1")
+    ts(T.x2[:], T.po[:], T.zw[:], T.wi[:], A.add, A.subtract, "po zw wi", "x2")
+    act(T.m1[:], ptw.indirect(T.x1[:]), "pt1 pt2 x1", "m1")
+    ts(T.o2[:, 0:8], T.fo[:], T.sr[:], None, A.add, None, "fo sr", "o2", grp="o2")
+    ts(T.o2[:, 8:16], T.fo[:], T.sr[:], 8.0, A.add, A.add, "fo sr", "o2", grp="o2")
+    tt(T.m2[:, 0:128], ptw.indirect(T.x2[:]), T.m2[:, 128:256], A.min, "pt1 pt2 x2 m2b", "m2a")
+    act(T.pm[:, 0:256], T.m2[:], "m2a m2b", "pm")
 
     for p in ask:
-        cp(T.rf[:, 48 * p:48 * p + 48], T.ans[:, p, :], [], ["rf"], grp="rf", ext=[("an%d" % p, arrivals(p))])
-    tt(T.ya[:], T.rf[:].indirect(T.o2[:]), T.m1[:], A.mult, ["rf", "rfp", "o2", "m1"], ["ya"])
-    ts(T.yb[:], T.ya[:], 0xFFF0, None, A.bitwise_and, None, ["ya"], ["yb"])
-    tt(T.pc[:, 0:128], T.yb[:, 0:128], T.pm[:, 0:128], A.mult, ["yb", "pm"], ["yc"], grp="yc")
-    tt(T.yc[:], T.yb[:, 128:256], T.pm[:, 128:256], A.mult, ["yb", "pm"], ["yc"], grp="yc")
-    tt(T.yd[:], T.yc[:], T.pc[:, 0:128], A.add, ["yc"], ["yd"])
-    ts(T.cu[:], T.yd[:], -0.5 + 2.0 ** -12, None, A.add, None, ["yd"], ["cu"])
-    for h in range(2):
+        cp(T.rf[:, 48 * p:48 * p + 48], T.ans[:, p, :], "", "rf", grp="rf", ext=[("an%d" % p, arrivals(p))])
+    tt(T.ya[:], T.rf[:].indirect(T.o2[:]), T.m1[:], A.mult, "rf rfp o2 m1", "ya")
+    ts(T.yb[:], T.ya[:], 0xFFF0, None, AND, None, "ya", "yb")
+    tt(T.pc[:, 0:128], T.yb[:, 0:128], T.pm[:, 0:128], A.mult, "yb pm", "yc", grp="yc")
+    tt(T.yc[:], T.yb[:, 128:256], T.pm[:, 128:256], A.mult, "yb pm", "yc", grp="yc")
+    tt(T.yd[:], T.yc[:], T.pc[:, 0:128], A.add, "yc", "yd")
+    ts(T.cu[:], T.yd[:], -0.5 + 2.0 ** -12, None, A.add, None, "yd", "cu")
+    for h, (a, b) in enumerate(((0, 10), (10, 16))):
         for c in range(8):
-            out = T.ob[:, 1024 * h + c:1024 * h + 1024:8]
-            src = T.dc[:].indirect(T.cu[:, 16 * c + 8 * h:16 * c + 8 * h + 8])
+            out = T.ob[:, 128 * a + c:128 * b:8]
+            src = T.dc[:].indirect(T.cu[:, 16 * c + a:16 * c + b])
             if c % 2 == 0:
-                cp(out, src, ["dc0", "dc1", "cu"], ["ov%d" % h], grp="ov%d" % h)
+                cp(out, src, "dc0 cu", "ov%d" % h, grp="ov%d" % h)
             else:
-                act(out, src, ["dc0", "dc1", "cu"], ["oa%d" % h], grp="oa%d" % h)
-        dma("s", T.y[:, 1024 * h:1024 * h + 1024], T.ob[:, 1024 * h:1024 * h + 1024], ["ov%d" % h, "oa%d" % h], ["y"], grp="y")
-    op("s", lambda q: None, ["y"], [], inc=0, ext=[("la", na), ("lq", nq), ("lw", nw)])
+                act(out, src, "dc0 cu", "oa%d" % h, grp="oa%d" % h)
+        dma("s", T.y[:, 128 * a:128 * b], T.ob[:, 128 * a:128 * b], "ov%d oa%d" % (h, h), "y", grp="y")
+    op("s", lambda q: None, "y", "", inc=0, ext=[("la", na), ("lq", nq), ("lw", nw)])
 
     emit(ops, {"g": g, "v": g.vector, "a": g.scalar, "s": g.sync, "t": g.tensor}, T)

@@ -1,26 +1,28 @@
 from concourse.bass import DstId, RemoteDMATransfer
 from concourse.mybir import AluOpType as A, AxisListType, ActivationFunctionType as AF
 
-N, S, HB, H0, ZB = 4, 2176, 512, 1536, 40
+N, S, HB, H0, ZB = 4, 2176, 512, 1536, 32
 WN, ZZ = S - HB, 3 * ZB
-RND = 402653184.0
+T2 = 496
+DH = 2048
+CH = ((0, 10), (10, 16))
 
-SCRATCH = {"wout": ("dram", [128, 2], "int32"), "win4": ("dram", [N, 128, 2], "int32"),
-           "msg": ("sbuf", [128, N, 4], "uint16"), "req": ("sbuf", [128, N, 4], "uint16"),
-           "rsp": ("sbuf", [128, N, 48], "uint16"), "ans": ("sbuf", [128, N, 48], "uint16")}
-for _t, _s in (("int32", "win:1664 wt:1 wdi:2 wall:8 pi:1 bi:4 ta:16 tb:16 cw:8 po:8 fo:8 ya:256 yb:256"),
-               ("uint16", "wdu:4 walu:8 wu:2 o1:34 x1:16 x2:8 x3:8 o2:16 cu:128"),
-               ("bfloat16", "dc:4096 ob:2048 t2:12 one:128 lh:128 rh:12"),
-               ("float32", "bf:4 ev:1 i16:16 tabq:128 isl:128 eh:40 ua:32 ub:32 utab:128 qc:12 tri:16 diag:16 qk:1 q32:1 "
-                           "z:16 eq:17 rk:1 ud:16 u:1 tab8:16 o32:32 tab2:16 w8:32 dx:32 inc:32 xs:33 gw:528 tw:1024 rf:200 "
-                           "pw:64 pt:240 k16:8 tz:16 wrep:128 zrep:128 wdg:16 zdg:16 wi:1 zw:1 sq:1 sr:1 ng:1 "
-                           "m1:256 m2:256 yc:128 yd:128")):
+SCRATCH = {"msg": ("sbuf", [128, N, 4], "uint16"), "req": ("sbuf", [128, N, 8], "uint16"),
+           "wall": ("sbuf", [128, N, 2], "int32"),
+           "rsp": ("sbuf", [128, N, 48], "uint16"), "ans": ("sbuf", [128, N, 48], "uint16"),
+           "o2": ("sbuf", [128, 2, 8], "uint16"), "x1": ("sbuf", [128, 2, 8], "uint16")}
+for _t, _s in (("int32", "win:1664 wt:1 pi:1 bi:5 qi:1 cw:8 fo:8 po:8 ya:256 yb:256"),
+               ("uint16", "wme:2 walu:8 wu:2 wb:2 o1:34 x2:8 x3:8 cu:128"),
+               ("bfloat16", "dc:4096 ob:2048 t2:16 one:128 lh:128 rh:16"),
+               ("float32", "i16:16 tabq:128 isl:128 eh:128 utab:128 tri:16 diag:16 nq:1 z:16 eq:21 rk:1 ud:16 u:1 "
+                           "d0:33 d1:32 xs:32 gw:544 tw:1040 rf:200 pt:192 tz:16 col:8 wrep:128 zrep:128 wdg:16 zdg:16 "
+                           "hf:32 wz:32 wi:1 zw:2 zz:1 k16:1 sq:1 sr:2 m1:256 ga:128 gb:128 yc:128 yd:128")):
     for _e in _s.split():
         SCRATCH[_e.split(":")[0]] = ("sbuf", [128, int(_e.split(":")[1])], _t)
-for _e in ("ps", "pm", "pc"):
+for _e in ("ps", "pm", "pn", "pc"):
     SCRATCH[_e] = ("psum", [128, 512], "float32")
-SEMAPHORES = (["s%d" % k for k in range(128)] + ["rq%d" % k for k in range(N)] + ["an%d" % k for k in range(N)]
-              + ["wq", "lw", "lq", "la"])
+SEMAPHORES = (["s%d" % k for k in range(136)] + ["rq%d" % k for k in range(N)] + ["an%d" % k for k in range(N)]
+              + ["lq", "la", "lw", "wq", "gq", "ga"])
 
 
 def emit(ops, queues, T):
@@ -100,8 +102,14 @@ def rank_program(g, core, T, topo):
     def red(out, a, r, w):
         op("v", lambda q: q.tensor_reduce(out, a, AxisListType.X, A.add), r, w)
 
-    def act(out, a, r, w, grp=None, **kw):
-        op("a", lambda q: q.activation(out, a, AF.Identity if kw else AF.Copy, **kw), r, w, grp=grp)
+    def scan(out, a, b, first, o0, o1, r, w):
+        op("v", lambda q: q.tensor_tensor_scan(out, a, b, first, o0, o1), r, w)
+
+    def turn(a, b, n, r, w):
+        op("v", lambda q: q.transpose(T.tw[:, a:a + n], T.gw[:, b:b + n]), r, w)
+
+    def act(out, a, r, w, grp=None, ext=(), **kw):
+        op("a", lambda q: q.activation(out, a, AF.Identity if kw else AF.Copy, **kw), r, w, grp=grp, ext=ext)
 
     def dma(qn, out, a, r, w, **kw):
         op(qn, lambda q: q.dma_start(out, a), r, w, inc=16, **kw)
@@ -118,152 +126,167 @@ def rank_program(g, core, T, topo):
     def arrivals(p):
         return len(topo.engines(T.cores[p], core))
 
-    p16, od, kk = T.bf[:, 0:1], T.bf[:, 1:2], T.bf[:, 2:3]
+    g16, p16, od, kk, pr = (T.eq[:, k:k + 1] for k in range(16, 21))
+    c16, s8, e1, o8 = (T.col[:, k:k + 1] for k in range(4))
     SHR, AND = A.logical_shift_right, A.bitwise_and
+    pt, wu, wdi, i8 = T.pt, T.wu[:, 0:1], T.wall[:, me, :], T.i16[:, 0:8]
 
     ms(T.win[:, H0:WN], 0, "wtail")
-    dma("a", T.wdi[:], T.wd[:], "", "wdi")
     dma("s", T.wt[:], T.want[:], "", "wt")
-    dma("a", T.wout[:], T.wd[:], "", "wout")
+    dma("a", wdi, T.wd[:], "", "wdi")
     for k in range(8):
-        dma("sa"[k % 2], T.win[k::16, 0:H0], T.strm[:, k:k + H0], "", "win", grp="win")
+        dma("sa"[k < 4], T.win[k::16, 0:H0], T.strm[:, k:k + H0], "", "win", grp="win")
     for k in range(8):
-        dma("as"[k < 5], T.win[8 + k::16, 0:WN - k], T.strm[:, HB + k:S], "wtail", "win", grp="win")
-    dma("s", T.dc[:], T.dic[:], "", "dc0")
+        dma("s", T.win[8 + k::16, 0:WN - k], T.strm[:, HB + k:S], "wtail", "win", grp="win")
 
-    op("g", lambda q: q.iota(T.pi[:], [[0, 1]], 0, 1), "", "pi")
+    op("g", lambda q: q.iota(T.pi[:], [[0, 1]], 0, 4), "", "pi")
     iota(T.i16[:], [[1, 16]], "i16")
-    iota(T.eh[:, 8:40], [[33, 2], [4, 8], [64, 2]], "eh")
-    iota(T.tabq[:], [[32, 4], [0, 32]], "tabq")
-    iota(T.qc[:], [[32, 4], [0, 3]], "qc")
-    iota(T.isl[:], [[16, 8], [0, 2], [1, 8]], "isl")
-    iota(T.t2[0:1, :], [[0, 4], [2, 3]], "t2")
+    iota(T.eh[:, 0:32], [[33, 2], [4, 8], [T2 // 8 + 4, 2]], "eh")
+    iota(T.isl[:, 0:16], [[0, 2], [1, 8]], "isl")
+    iota(T.t2[0:1, :], [[0, 4], [2, 4]], "t2")
 
     far = [topo.addr(T.cores[p]) for p in ask]
     wtr = RemoteDMATransfer(dst_ids=[DstId(rid=a[0], pnc=a[1]) for a in far], dma_engine_mask=topo.mask(core, T.cores[ask[0]]),
-                            remote_sem=T.sem.wq, srcs=[T.wout[:]], dsts=[T.win4[me] for _ in far])
-    op("g", lambda q: q.remote_dma_fused([wtr], local_sem=T.sem.lw), "wout", "", inc=0)
+                            remote_sem=T.sem.wq, srcs=[wdi], dsts=[wdi for _ in far])
+    op("g", lambda q: q.remote_dma_fused([wtr], local_sem=T.sem.lw), "wdi", "", inc=0)
     nw = len(topo.engines(core, T.cores[ask[0]]))
+    iota(T.tz[:], [[0, 8], [ZZ, 2]], "tz")
 
-    act(T.tab8[:], T.i16[:], "i16", "tab8", scale=8.0)
-    act(T.o32[:], T.eh[:, 8:40], "eh", "o32", scale=0.0, bias=1.0)
-    act(T.one[0:1, :], T.tabq[0:1, :], "tabq", "one", scale=0.0, bias=1.0)
-    ms(T.eh[:, 7:8], 124.0, "eh0")
-    ts(T.bi[:, 0:1], T.pi[:], 15, None, AND, None, "pi", "bi", grp="bi")
-    ts(T.bi[:, 1:2], T.pi[:], 4, 1, SHR, AND, "pi", "bi", grp="bi")
-    ts(T.bi[:, 2:3], T.pi[:], 3, 1, SHR, AND, "pi", "bi", grp="bi")
-    cp(T.bf[:, 0:3], T.bi[:, 0:3], "bi", "bf")
-    ts(T.ta[:], T.i16[:], p16, None, A.mult, None, "i16 bf", "ta")
-    ts(T.ev[:], od, -1.0, 1.0, A.mult, A.add, "bf", "ev")
-    ts(T.ub[:], T.eh[:, 7:39], 2.0, od, A.add, A.mult, "bf eh eh0", "ub")
-    ts(T.tb[:], T.ta[:], 1, None, SHR, None, "ta", "tb")
-    ts(T.ua[:], T.eh[:, 8:40], T.ev[:], None, A.mult, None, "ev eh", "ua")
-    ts(T.ub[:, 16:17], T.ub[:, 16:17], od, None, A.add, None, "ub bf", "ub")
-    ts(T.tri[:], T.i16[:], p16, 1024.0, A.is_ge, A.mult, "bf i16", "tri")
-    ts(T.diag[:], T.i16[:], p16, None, A.is_equal, None, "bf i16", "diag")
-    ts(T.eq[:, 16:17], T.pi[:], p16, None, A.subtract, None, "pi bf", "g16")
+    ms(T.hf[:], 0.5, "hf")
+    ms(T.one[0:1, :], 1.0, "one")
+    ms(T.o1[:], 0, "o1z")
+    ts(T.bi[:, 0:1], T.pi[:], 2, 0x70, SHR, AND, "pi", "bi", grp="bi")
+    ts(T.bi[:, 1:2], T.pi[:], 2, 15, SHR, AND, "pi", "bi", grp="bi")
+    ts(T.bi[:, 2:3], T.pi[:], 64, None, AND, None, "pi", "bi", grp="bi")
+    ts(T.bi[:, 3:4], T.pi[:], 5, 1, SHR, AND, "pi", "bi", grp="bi")
+    ts(T.bi[:, 4:5], T.pi[:], 2, 1, SHR, AND, "pi", "bi", grp="bi")
+    ms(T.d0[:], 0.0, "d0")
+    ms(T.rf[:, 192:200], 0.0, "rfp")
+    cp(T.eq[:, 16:21], T.bi[:], "bi", "bf")
+    scan(pt[:, 0:32], T.hf[:], T.d0[:, 0:32], 2.0, A.mult, A.add, "hf d0", "pw")
+    op("t", lambda q: q.matmul(T.ps[:, 0:16], T.one[0:1, :], T.t2[0:1, :], True, False), "one t2", "", inc=0)
     for q in range(N):
-        tt(T.utab[:, 32 * q:32 * q + 32], T.ua[:], T.ub[:], A.add, "ua ub", "utab", grp="utab")
-    tt(T.tab2[:], T.tb[:], T.tab8[:], A.subtract, "tb tab8", "tab2")
-    op("t", lambda q: q.matmul(T.ps[:, 0:12], T.one[0:1, :], T.t2[0:1, :], True, False), "one t2", "", inc=0)
+        act(T.tabq[:, 32 * q:32 * q + 32], T.hf[:], "hf", "tabq", grp="tabq", scale=0.0, bias=-32.0 * q)
+    for n in (16, 32):
+        act(T.eh[:, 2 * n:4 * n], T.eh[:, 0:2 * n], "eh", "eh")
+        act(T.isl[:, n:2 * n], T.isl[:, 0:n], "isl", "isl", bias=float(n))
 
-    wu = T.wu[:, 0:1]
-    cp(T.wdu[:, 0:4:2], T.wdi[:], "wdi", "wdu")
-    for h in range(2):
-        act(T.w8[:, 16 * h:16 * h + 16], T.tab8[:].indirect(T.wdu[:, 2 * h:2 * h + 1]), "tab8 wdu", "w8", grp="w8")
-    for h in range(2):
-        act(T.dx[:, 16 * h:16 * h + 16], T.tab2[:].indirect(T.wdu[:, 2 * h:2 * h + 1]), "tab2 wdu", "dx", grp="dx",
-            bias=-float(HB * h))
-    act(T.xs[:, 32:33], T.dx[:, 0:1], "dx w8", "xs0", bias=T.w8[:, 0:1])
+    cp(T.wme[:], wdi, "wdi", "wme")
+    ts(c16, p16, -1.0, 16.0, A.mult, A.add, "bf", "c16")
     cp(wu, T.wt[:], "wt", "wu")
-    ts(T.qk[:], T.wt[:], -15.5, RND, A.add, A.add, "wt", "qk")
+    act(T.d1[:], T.i16[:].indirect(T.wme[:]), "i16 wme bf", "d1", scale=p16)
+    act(T.d0[:, 1:33], T.i16[:].indirect(T.wme[:]), "i16 wme c16", "d0", scale=c16)
+    act(T.isl[:, 64:128], T.isl[:, 0:64], "isl", "isl", bias=64.0)
+    ts(T.tri[:], T.i16[:], p16, 1024.0, A.is_ge, A.mult, "bf i16", "tri")
+    ts(T.qi[:], T.wt[:], 1.0 / 32, -15.5 / 32, A.mult, A.add, "wt", "qi")
+    ts(T.utab[:, 0:128:2], T.eh[:, 0:128:2], od, None, A.add, None, "eh bf", "utab", grp="utab")
     tt(T.z[:], T.tabq[:].indirect(wu), T.tri[:], A.add, "tabq wu tri", "z")
-    ts(T.q32[:], T.qk[:], -RND, None, A.add, None, "qk", "q32")
+    ts(T.nq[:], T.qi[:], -32.0, None, A.mult, None, "qi", "nq")
+    ts(T.utab[:, 1:128:2], T.eh[:, 1:128:2], od, None, A.subtract, None, "eh bf", "utab", grp="utab")
+    ts(T.diag[:], T.i16[:], p16, None, A.is_equal, None, "bf i16", "diag")
+    scan(T.xs[:], T.d0[:, 0:32], T.d1[:], 0.0, A.add, A.add, "d0 d1", "xs")
+    ts(T.eq[:, 0:16], T.z[:], T.nq[:], None, A.is_equal, None, "z nq", "eq")
     tt(T.ud[:], T.utab[:].indirect(wu), T.diag[:], A.mult, "utab wu diag", "ud")
-    ts(T.eq[:, 0:16], T.z[:], T.q32[:], None, A.is_equal, None, "z q32", "eq")
-    op("v", lambda q: q.tensor_tensor_scan(T.inc[:], T.o32[:], T.w8[:], 0.0, A.mult, A.add), "o32 w8", "inc")
-    red(T.rk[:], T.eq[:], "eq g16", "rk")
+    ts(T.o1[:, 17:33], T.xs[:, 16:32], 0.5, -HB - 0.25, A.mult, A.add, "xs o1z", "o1", grp="o1")
+    red(T.rk[:], T.eq[:, 0:17], "eq bf", "rk")
     red(T.u[:], T.ud[:], "ud", "u")
+    ts(T.o1[:, 1:17], T.xs[:, 0:16], 0.5, -0.25, A.mult, A.add, "xs o1z", "o1", grp="o1")
     ts(T.lh[:], T.isl[:], T.rk[:], 8.0, A.is_equal, A.mult, "isl rk", "lh")
-    ts(T.rh[:], T.qc[:], T.q32[:], T.u[:], A.is_equal, A.mult, "qc q32 u", "rh")
-    op("t", lambda q: q.matmul(T.ps[:, 0:12], T.lh[:], T.rh[:], False, True), "lh rh", "ps")
-    tt(T.xs[:, 0:32], T.dx[:], T.inc[:], A.add, "dx inc", "xs")
-    cp(T.o1[:, 0:33], T.xs[:], "xs xs0", "o1")
-    ts(T.msg[:, :, 0:3], T.ps[:, 0:12], kk, None, A.add, None, "ps bf", "msgl")
+    ts(T.rh[:], T.tabq[:, 0:128:8], T.nq[:], T.u[:], A.is_equal, A.mult, "tabq nq u", "rh")
+    op("t", lambda q: q.matmul(T.ps[:, 0:16], T.lh[:], T.rh[:], False, True), "lh rh", "ps")
+    ts(T.sq[:], T.nq[:], -1.5, T.rk[:], A.mult, A.add, "nq rk", "sq")
+
+    act(s8, pr, "bf", "col", grp="col", scale=2.0 ** -8 - 1.0, bias=1.0)
+    act(e1, pr, "bf", "col", grp="col", scale=-1.0, bias=1.0)
+    act(o8, pr, "bf", "col", grp="col", scale=256.0)
+    act(pt[:, 32:49], pt[:, 0:17], "pw", "pa", grp="pa", scale=65536.0)
+    act(pt[:, 81:96], pt[:, 17:32], "pw", "pa", grp="pa", scale=2.0 ** 32)
+    act(pt[:, 96:104], pt[:, 0:8], "pw col", "pt", grp="pt", scale=s8)
+    act(pt[:, 104:128], pt[:, 8:32], "pw col", "pt", grp="pt", scale=e1)
+    act(pt[:, 128:137], pt[:, 32:41], "pa col", "pt", grp="pt", scale=s8)
+    act(pt[:, 137:145], pt[:, 41:49], "pa col bf", "pt", grp="pt", scale=e1, bias=pr)
+    act(pt[:, 169:177], pt[:, 41:49], "pa col", "pt", grp="pt", scale=o8)
+    act(pt[:, 177:192], pt[:, 81:96], "pa col", "pt", grp="pt", scale=s8)
+
+    cp(T.gw[:, 0:256], T.win[:].indirect(T.o1[:, 0:16]), "win wtail o1", "gwa")
+    act(T.gw[:, 256:544], T.win[:].indirect(T.o1[:, 16:34]), "win wtail o1", "gwb")
+    ts(T.msg[:], T.ps[:, 0:16], kk, None, A.add, None, "ps bf", "msgl")
     nq = sum(send(T.msg[:, p, 0:3], T.req[:, me, 0:3], "rq", "lq", p, "msgl") for p in ask)
-    iota(T.tz[:], [[2, 8], [ZZ + 1, 2]], "tz")
-
-    cp(T.gw[:], T.win[:].indirect(T.o1[:, 0:33]), "win wtail o1", "gw")
-    op("v", lambda q: q.transpose(T.tw[:, 0:512], T.gw[:, 0:512]), "gw", "tw", grp="tw")
-    op("v", lambda q: q.transpose(T.tw[:, 512:1024], T.gw[:, 16:528]), "gw", "tw", grp="tw")
-
-    act(T.pw[:, 0:1], T.i16[:, 0:1], "i16", "pw", bias=1.0)
-    act(T.ng[:], T.eq[:, 16:17], "g16", "ng", scale=-1.0)
-    for j in range(6):
-        n = 1 << j
-        act(T.pw[:, n:2 * n], T.pw[:, 0:n], "pw", "pw", scale=2.0 ** -n)
-        if j == 0:
-            act(T.sq[:], T.q32[:], "q32 rk", "sq", scale=1.5, bias=T.rk[:])
-        if j == 1:
-            act(T.k16[:], T.i16[:, 0:8], "i16", "k16", scale=0.0, bias=16.0)
-        if j == 2:
-            act(T.sr[:], T.sq[:], "sq ng", "sr", bias=T.ng[:])
-        if j == 3:
-            act(T.rf[:, 192:200], T.i16[:, 0:8], "i16", "rfp", scale=0.0)
-    for a, b, c, s, o in ((0, 16, 0, 1.0, 0.0), (16, 40, 16, 0.0, 0.0), (40, 57, 0, 65536.0, 0.0), (57, 80, 17, 0.0, 1.0),
-                          (80, 97, 0, 0.0, 0.0), (97, 120, 17, 4294967296.0, 0.0), (232, 240, 0, 0.0, 0.0)):
-        act(T.pt[:, a:b], T.pw[:, c:c + b - a], "pw", "pt1", grp="pt1", scale=s, bias=o)
-    dma("s", T.wall[:, 2 * me:2 * me + 2], T.wd[:], "", "wall", grp="wall")
-    for p in tell:
-        dma("s", T.wall[:, 2 * p:2 * p + 2], T.win4[p], "", "wall", grp="wall", ext=[("wq", sum(arrivals(r) for r in tell))])
-    dma("a", T.pt[0::2, ZZ:2 * ZZ - 8], T.pt[0::2, 0:ZZ - 8], "pt1", "pt2", grp="pt2")
-    dma("a", T.pt[1::2, ZZ:2 * ZZ - 8], T.pt[1::2, 8:ZZ], "pt1", "pt2", grp="pt2")
-
-    na = 0
-    for p in tell:
-        cp(T.rsp[:, p, :], T.tw[:].indirect(T.req[:, p, 0:3]), "tw", "rsp%d" % p, ext=[("rq%d" % p, arrivals(p))])
-        na += send(T.rsp[:, p, :], T.ans[:, me, :], "an", "la", p, "rsp%d" % p)
-
-    ptw = T.pt[:]
-    cp(T.walu[:], T.wall[:], "wall", "walu")
+    op("g", lambda q: q.sem_inc(T.sem.gq, 1), "", "", inc=0)
+    dma("s", T.dc[:, 0:DH], T.dic[:, 0:DH], "", "dc", grp="dc", ext=[("gq", 1)])
+    ts(T.sr[:, 0:1], T.sq[:], g16, None, A.subtract, None, "sq bf", "sr", grp="sr")
+    ts(T.sr[:, 1:2], T.sq[:], g16, 8.0, A.subtract, A.add, "sq bf", "sr", grp="sr")
+    act(T.walu[:], T.wall[:], "wdi", "walu", ext=[("wq", sum(arrivals(r) for r in tell))])
+    for a, b, v in ((49, 64, 1.0), (64, 81, 0.0), (145, 160, 1.0)):
+        act(pt[:, a:b], pt[:, 0:b - a], "pw", "pt", grp="pt", scale=0.0, bias=v)
     act(T.wrep[:], T.i16[:].indirect(T.walu[:]), "i16 walu", "wrep")
     act(T.zrep[:], T.tz[:].indirect(T.walu[:]), "tz walu", "zrep")
-    cp(T.rf[:, 48 * me:48 * me + 48], T.tw[:].indirect(T.msg[:, me, 0:3]), "tw msgl", "rf", grp="rf")
+    act(pt[:, 160:169], pt[:, 0:9], "pw", "pt", grp="pt", scale=0.0)
+    turn(T2, 0, 256, "gwa", "twa")
+    turn(T2 + 256, 256, 288, "gwb", "twb")
+    turn(0, 16, 512, "gwa gwb", "twa")
+
+    def answer(p):
+        cp(T.rsp[:, p, :], T.tw[:].indirect(T.req[:, p, 0:3]), "twa twb", "rsp%d" % p, ext=[("rq%d" % p, arrivals(p))])
+        return send(T.rsp[:, p, :], T.ans[:, me, :], "an", "la", p, "rsp%d" % p)
+
     tt(T.wdg[:], T.wrep[:].indirect(wu), T.diag[:], A.mult, "wrep wu diag", "wdg")
-    red(T.wi[:], T.wdg[:], "wdg", "wi")
-    ts(T.cw[:], T.i16[:, 0:8], T.wi[:], None, A.mult, None, "i16 wi", "cw")
-    ts(T.x3[:], T.k16[:], T.wi[:], None, A.subtract, None, "k16 wi", "x3")
     tt(T.zdg[:], T.zrep[:].indirect(wu), T.diag[:], A.mult, "zrep wu diag", "zdg")
+    act(T.wz[:, 0:16], T.wdg[:], "wdg", "wi", accum_out=T.wi[:])
+    act(T.wz[:, 16:32], T.zdg[:], "zdg", "zz", accum_out=T.zz[:])
+    act(T.cw[:], i8, "i16 wi", "cw", scale=T.wi[:])
+    act(T.k16[:], T.wi[:], "wi", "k16", scale=-1.0, bias=16.0)
+    act(T.zw[:, 0:1], T.zz[:], "zz wi", "zw0", bias=T.wi[:])
+    na = sum(answer(p) for p in tell)
+    op("g", lambda q: q.sem_inc(T.sem.ga, 1), "", "", inc=0)
+    dma("s", T.dc[:, DH:], T.dic[:, DH:], "", "dc", grp="dc", ext=[("ga", 1)])
     ts(T.po[:], T.cw[:], 15, None, AND, None, "cw", "po")
-    red(T.zw[:], T.zdg[:], "zdg", "zw")
-    act(T.m2[:, 128:256], ptw.indirect(T.x3[:]), "pt1 pt2 x3", "m2b")
     ts(T.fo[:], T.cw[:], 1, 0x78, SHR, AND, "cw", "fo")
-    ts(T.x1[:, 0:8], T.po[:], T.zw[:], float(ZB), A.add, A.add, "po zw", "x1", grp="x1")
-    ts(T.x1[:, 8:16], T.po[:], T.zw[:], float(2 * ZB), A.add, A.add, "po zw", "x1", grp="x1")
-    ts(T.x2[:], T.po[:], T.zw[:], T.wi[:], A.add, A.subtract, "po zw wi", "x2")
-    act(T.m1[:], ptw.indirect(T.x1[:]), "pt1 pt2 x1", "m1")
-    ts(T.o2[:, 0:8], T.fo[:], T.sr[:], None, A.add, None, "fo sr", "o2", grp="o2")
-    ts(T.o2[:, 8:16], T.fo[:], T.sr[:], 8.0, A.add, A.add, "fo sr", "o2", grp="o2")
-    tt(T.m2[:, 0:128], ptw.indirect(T.x2[:]), T.m2[:, 128:256], A.min, "pt1 pt2 x2 m2b", "m2a")
-    act(T.pm[:, 0:256], T.m2[:], "m2a m2b", "pm")
+    act(T.x3[:], i8, "i16 k16", "x3", scale=0.0, bias=T.k16[:])
+    cp(T.rf[:, 48 * me:48 * me + 48], T.tw[:].indirect(T.msg[:, me, 0:3]), "twa twb msgl", "rf", grp="rf")
+    for t in range(2):
+        ts(T.x1[:, :, 4 * t:4 * t + 4], T.po[:], T.zw[:, 0:1], float(ZB * t), A.add, A.add, "po zw0", "x1", grp="x1")
+    ts(T.x2[:], T.po[:], T.zz[:], None, A.add, None, "po zz", "x2")
+    act(T.gb[:], pt[:, 0:32].indirect(T.x3[:]), "pw x3", "gb")
+    act(T.m1[:, 0:128], pt[:, ZB:].indirect(T.x1[:, 0, :]), "pa pt x1", "m10")
+    act(T.m1[:, 128:256], pt[:, ZB:].indirect(T.x1[:, 1, :]), "pa pt x1", "m11")
+    for t in range(2):
+        ts(T.o2[:, :, 4 * t:4 * t + 4], T.fo[:], T.sr[:, t:t + 1], None, A.add, None, "fo sr", "o2", grp="o2")
+    tt(T.ga[:], pt[:].indirect(T.x2[:]), T.gb[:], A.min, "pw pa pt x2 gb", "ga")
+    act(T.pn[:, 0:128], T.gb[:], "gb", "pn")
+    act(T.pm[:, 0:128], T.ga[:], "ga", "pm")
 
     for p in ask:
         cp(T.rf[:, 48 * p:48 * p + 48], T.ans[:, p, :], "", "rf", grp="rf", ext=[("an%d" % p, arrivals(p))])
-    tt(T.ya[:], T.rf[:].indirect(T.o2[:]), T.m1[:], A.mult, "rf rfp o2 m1", "ya")
-    ts(T.yb[:], T.ya[:], 0xFFF0, None, AND, None, "ya", "yb")
-    tt(T.pc[:, 0:128], T.yb[:, 0:128], T.pm[:, 0:128], A.mult, "yb pm", "yc", grp="yc")
-    tt(T.yc[:], T.yb[:, 128:256], T.pm[:, 128:256], A.mult, "yb pm", "yc", grp="yc")
-    tt(T.yd[:], T.yc[:], T.pc[:, 0:128], A.add, "yc", "yd")
-    ts(T.cu[:], T.yd[:], -0.5 + 2.0 ** -12, None, A.add, None, "yd", "cu")
-    for h, (a, b) in enumerate(((0, 10), (10, 16))):
+
+    def step(k, h):
+        c, j = slice(128 * h, 128 * h + 128), slice(64 * h, 64 * h + 64)
+        ca, cb = slice(128 * h, 128 * h + 64), slice(128 * h + 64, 128 * h + 128)
+        if k == 0:
+            tt(T.ya[:, c], T.rf[:].indirect(T.o2[:, h, :]), T.m1[:, c], A.mult, "rf rfp o2 m1%d" % h, "ya%d" % h)
+        if k == 1:
+            ts(T.yb[:, c], T.ya[:, c], 0xFFF0, None, AND, None, "ya%d" % h, "yb%d" % h)
+        if k == 2:
+            tt(T.yc[:, j], T.yb[:, cb], T.pn[:, j], A.mult, "yb%d pn" % h, "yc%d" % h, grp="yc%d" % h)
+            tt(T.pc[:, j], T.yb[:, ca], T.pm[:, j], A.mult, "yb%d pm" % h, "yc%d" % h, grp="yc%d" % h)
+        if k == 3:
+            tt(T.yd[:, j], T.yc[:, j], T.pc[:, j], A.add, "yc%d" % h, "yd%d" % h)
+        if k == 4:
+            ts(T.cu[:, j], T.yd[:, j], -0.5 + 2.0 ** -12, None, A.add, None, "yd%d" % h, "cu%d" % h)
+
+    for k in range(5):
+        for h in range(2):
+            step(k, h)
+
+    for h, (a, b) in enumerate(CH):
         for c in range(8):
             out = T.ob[:, 128 * a + c:128 * b:8]
             src = T.dc[:].indirect(T.cu[:, 16 * c + a:16 * c + b])
-            if c % 2 == 0:
-                cp(out, src, "dc0 cu", "ov%d" % h, grp="ov%d" % h)
+            if c >= 4:
+                cp(out, src, "dc cu1", "ov%d" % h, grp="ov%d" % h)
             else:
-                act(out, src, "dc0 cu", "oa%d" % h, grp="oa%d" % h)
+                act(out, src, "dc cu0", "oa%d" % h, grp="oa%d" % h)
         dma("s", T.y[:, 128 * a:128 * b], T.ob[:, 128 * a:128 * b], "ov%d oa%d" % (h, h), "y", grp="y")
-    op("s", lambda q: None, "y", "", inc=0, ext=[("la", na), ("lq", nq), ("lw", nw)])
+    op("s", lambda q: None, "y", "", inc=0, ext=[("lq", nq), ("la", na), ("lw", nw)])
 
     emit(ops, {"g": g, "v": g.vector, "a": g.scalar, "s": g.sync, "t": g.tensor}, T)

@@ -1,28 +1,34 @@
-from concourse.bass import DstId, RemoteDMATransfer
 from concourse.mybir import AluOpType as A, AxisListType, ActivationFunctionType as AF
 
-N, S, HB, H0, ZB = 4, 2176, 512, 1536, 32
-WN, ZZ = S - HB, 3 * ZB
+N, S = 4, 2176
+X, W0, WN = 512, 1536, 1664
 T2 = 496
-DH = 2048
+GW = (0, 6, 18, 34)
+DC = (0, 1024, 2560, 4096)
 CH = ((0, 10), (10, 16))
 
-SCRATCH = {"msg": ("sbuf", [128, N, 4], "uint16"), "req": ("sbuf", [128, N, 8], "uint16"),
-           "wall": ("sbuf", [128, N, 2], "int32"),
+ORDER = {"v": "wtail d0z zr hf bi pw o1z bf n16 bq tri ute diag uto z bu po d1 eq ud xf key u xe xs lh rh o1 b0 c256 "
+              "gw0 msg tmx pb tw0b tw1b tw0a tw1a tw2a tw2b wr0 rsp0 wdg rsp2 wi td o3 o5 m11 rf0 rf2 "
+              "ya0 ya1 yb0 yb1 sc0 sc1 cu0 cu1 l03 l04 l05 l06 l11 l13 l14 l15 l16",
+         "a": "wt win i6 wme qu e1 cw c16 q6 wz s8 d0 wm2 pw2 wu y16 gw1 gw2 wr3 ta b1 wfu tmy wr2 wr1 rsp1 rfme o2 m10 d20 "
+              "rf1 d21 d2f"}
+
+ONE, NIL = 1.0, 0.0
+SCRATCH = {"msg": ("sbuf", [128, N, 8], "uint16"), "req": ("sbuf", [128, N, 8], "uint16"),
            "rsp": ("sbuf", [128, N, 48], "uint16"), "ans": ("sbuf", [128, N, 48], "uint16"),
-           "o2": ("sbuf", [128, 2, 8], "uint16"), "x1": ("sbuf", [128, 2, 8], "uint16")}
-for _t, _s in (("int32", "win:1664 wt:1 pi:1 bi:5 qi:1 cw:8 fo:8 po:8 ya:256 yb:256"),
-               ("uint16", "wme:2 walu:8 wu:2 wb:2 o1:34 x2:8 x3:8 cu:128"),
-               ("bfloat16", "dc:4096 ob:2048 t2:16 one:128 lh:128 rh:16"),
-               ("float32", "i16:16 tabq:128 isl:128 eh:128 utab:128 tri:16 diag:16 nq:1 z:16 eq:21 rk:1 ud:16 u:1 "
-                           "d0:33 d1:32 xs:32 gw:544 tw:1040 rf:200 pt:192 tz:16 col:8 wrep:128 zrep:128 wdg:16 zdg:16 "
-                           "hf:32 wz:32 wi:1 zw:2 zz:1 k16:1 sq:1 sr:2 m1:256 ga:128 gb:128 yc:128 yd:128")):
+           "o2": ("sbuf", [128, 2, 8], "uint16"), "o3": ("sbuf", [128, 2, 8], "uint16")}
+for _t, _s in (("int32", "win:1664 wt:1 wdi:2 wfar:2 pi:1 bi:5 bq:1 cw:9 po:9 ya:256 yb:256"),
+               ("uint16", "wfu:2 qu:2 wu:2 bu:2 o1:34 xe:10 o5:8 cu:128"),
+               ("bfloat16", "dc:4096 ob:2048 isl:144 lh:144 rh:24"),
+               ("float32", "i32:24 i6:8 wz:10 bf:5 y16:144 col:8 hf:32 zr:32 pw:64 xf:9 tri:16 diag:16 z:16 eq:17 u:1 key:1 "
+                           "d0:33 d1:32 xs:32 eh:16 ut:32 ud:16 c256:8 n16:8 gw:544 tw:1040 rf:192 tm:144 ta:72 wrep:128 wdg:16 "
+                           "wi:1 m1:256 d2:256 sc:256")):
     for _e in _s.split():
         SCRATCH[_e.split(":")[0]] = ("sbuf", [128, int(_e.split(":")[1])], _t)
-for _e in ("ps", "pm", "pn", "pc"):
+for _e in ("ps", "pb"):
     SCRATCH[_e] = ("psum", [128, 512], "float32")
-SEMAPHORES = (["s%d" % k for k in range(136)] + ["rq%d" % k for k in range(N)] + ["an%d" % k for k in range(N)]
-              + ["lq", "la", "lw", "wq", "gq", "ga"])
+SEMAPHORES = (["s%d" % k for k in range(130)] + ["%s%d" % (s, k) for s in ("rq", "an", "wq") for k in range(N)]
+              + ["lq", "la", "lw", "gq", "ga"])
 
 
 def emit(ops, queues, T):
@@ -51,8 +57,14 @@ def emit(ops, queues, T):
             total[key[n]] = total.get(key[n], 0) + o["inc"]
             if key[n] not in sem:
                 sem[key[n]] = T.sem["s%d" % len(sem)]
+
+    def place(n):
+        names = ORDER.get(ops[n]["q"], "").split()
+        return (names.index(ops[n]["name"]) if ops[n]["name"] in names else len(names), n)
+
     done = {}
-    for n, o in enumerate(ops):
+    for n in sorted(range(len(ops)), key=place):
+        o = ops[n]
         q = queues[o["q"]]
         seen = done.setdefault(o["q"], set())
         for k in sorted(set(key[m] for m in deps[n]), key=str):
@@ -81,8 +93,9 @@ def rank_program(g, core, T, topo):
     tell = [(me - d) % N for d in steps]
     ops = []
 
-    def op(q, f, r, w, grp=None, inc=1, ext=()):
-        ops.append({"q": q, "f": f, "r": r.split(), "w": w.split(), "grp": grp, "inc": inc, "ext": list(ext)})
+    def op(q, f, r, w, grp=None, inc=1, ext=(), name=None):
+        ops.append({"q": q, "f": f, "r": r.split(), "w": w.split(), "grp": grp, "inc": inc, "ext": list(ext),
+                    "name": name or w})
 
     def ts(out, in0, s1, s2, o0, o1, r, w, **kw):
         if o1 is None:
@@ -93,29 +106,33 @@ def rank_program(g, core, T, topo):
     def tt(out, a, b, o, r, w, **kw):
         op("v", lambda q: q.tensor_tensor(out, a, b, o), r, w, **kw)
 
-    def cp(out, a, r, w, **kw):
-        op("v", lambda q: q.tensor_copy(out, a), r, w, **kw)
-
     def ms(out, c, w):
         op("v", lambda q: q.memset(out, c), "", w)
 
     def red(out, a, r, w):
         op("v", lambda q: q.tensor_reduce(out, a, AxisListType.X, A.add), r, w)
 
-    def scan(out, a, b, first, o0, o1, r, w):
-        op("v", lambda q: q.tensor_tensor_scan(out, a, b, first, o0, o1), r, w)
+    def scan(out, a, b, first, o0, o1, r, w, **kw):
+        op("v", lambda q: q.tensor_tensor_scan(out, a, b, first, o0, o1), r, w, **kw)
 
-    def turn(a, b, n, r, w):
-        op("v", lambda q: q.transpose(T.tw[:, a:a + n], T.gw[:, b:b + n]), r, w)
+    def turn(a, b, n, r, w, **kw):
+        op("v", lambda q: q.transpose(T.tw[:, a:a + n], T.gw[:, b:b + n]), r, w, **kw)
 
-    def act(out, a, r, w, grp=None, ext=(), **kw):
-        op("a", lambda q: q.activation(out, a, AF.Identity if kw else AF.Copy, **kw), r, w, grp=grp, ext=ext)
+    def act(out, a, r, w, scale=ONE, bias=NIL, **kw):
+        plain = scale is ONE and bias is NIL
+        if kw.get("name", w) not in ORDER["v"].split():
+            op("a", lambda q: q.activation(out, a, AF.Copy if plain else AF.Identity, bias=bias, scale=scale), r, w, **kw)
+        elif plain:
+            op("v", lambda q: q.tensor_copy(out, a), r, w, **kw)
+        else:
+            ts(out, a, scale, bias, A.mult, A.add, r, w, **kw)
+        ops[-1]["flex"] = True
 
     def dma(qn, out, a, r, w, **kw):
         op(qn, lambda q: q.dma_start(out, a), r, w, inc=16, **kw)
 
-    def iota(out, pat, w):
-        op("g", lambda q: q.iota(out, pat, 0, 0, allow_small_or_imprecise_dtypes=True), "", w)
+    def iota(out, pat, w, base=0, ch=0):
+        op("g", lambda q: q.iota(out, pat, base, ch, allow_small_or_imprecise_dtypes=True), "", w)
 
     def send(src, dst, sem, local, p, r):
         rid, pid, _ = topo.addr(T.cores[p])
@@ -123,170 +140,144 @@ def rank_program(g, core, T, topo):
                                        topo.mask(core, T.cores[p])), r, "", inc=0)
         return len(topo.engines(core, T.cores[p]))
 
-    def arrivals(p):
-        return len(topo.engines(T.cores[p], core))
+    def landed(sem, p):
+        return [("%s%d" % (sem, p), len(topo.engines(T.cores[p], core)))]
 
-    g16, p16, od, kk, pr = (T.eq[:, k:k + 1] for k in range(16, 21))
-    c16, s8, e1, o8 = (T.col[:, k:k + 1] for k in range(4))
+    def book(k, sem=None):
+        if DC[k] < DC[k + 1]:
+            if sem:
+                op("g", lambda q: q.sem_inc(T.sem[sem], 1), "", "", inc=0)
+            dma("s", T.dc[:, DC[k]:DC[k + 1]], T.dic[:, DC[k]:DC[k + 1]], "", "dc", grp="dc", ext=[(sem, 1)] if sem else [])
+
+    pp, pr, c8, che, od = (T.bf[:, k:k + 1] for k in range(5))
+    s8, b0, b1, e1, c16 = (T.col[:, k:k + 1] for k in range(5))
     SHR, AND = A.logical_shift_right, A.bitwise_and
-    pt, wu, wdi, i8 = T.pt, T.wu[:, 0:1], T.wall[:, me, :], T.i16[:, 0:8]
+    wme, wu, qu, bu, q6 = T.msg[:, ask[0], 0:2], T.wu[:, 0:1], T.qu[:, 0:1], T.bu[:, 0:1], T.eq[:, 16:17]
+    yv, zv = T.y16[:, 0::2], T.y16[:, 1::2]
+    FLOOR = -0.5 + 2.0 ** -12
 
-    ms(T.win[:, H0:WN], 0, "wtail")
-    dma("s", T.wt[:], T.want[:], "", "wt")
-    dma("a", wdi, T.wd[:], "", "wdi")
+    ms(T.win[:, W0:WN], 0, "wtail")
+    dma("s", T.wdi[:], T.wd[:], "", "wdi")
+    dma("a", T.wt[:], T.want[:], "", "wt")
     for k in range(8):
-        dma("sa"[k < 4], T.win[k::16, 0:H0], T.strm[:, k:k + H0], "", "win", grp="win")
+        dma("sa"[k < 4], T.win[k::16, 0:W0], T.strm[:, k:k + W0], "", "win", grp="win")
     for k in range(8):
-        dma("s", T.win[8 + k::16, 0:WN - k], T.strm[:, HB + k:S], "wtail", "win", grp="win")
+        dma("s", T.win[8 + k::16, 0:WN - k], T.strm[:, X + k:S], "wtail", "win", grp="win")
+    book(0)
 
     op("g", lambda q: q.iota(T.pi[:], [[0, 1]], 0, 4), "", "pi")
-    iota(T.i16[:], [[1, 16]], "i16")
-    iota(T.eh[:, 0:32], [[33, 2], [4, 8], [T2 // 8 + 4, 2]], "eh")
-    iota(T.isl[:, 0:16], [[0, 2], [1, 8]], "isl")
-    iota(T.t2[0:1, :], [[0, 4], [2, 4]], "t2")
-
-    far = [topo.addr(T.cores[p]) for p in ask]
-    wtr = RemoteDMATransfer(dst_ids=[DstId(rid=a[0], pnc=a[1]) for a in far], dma_engine_mask=topo.mask(core, T.cores[ask[0]]),
-                            remote_sem=T.sem.wq, srcs=[wdi], dsts=[wdi for _ in far])
-    op("g", lambda q: q.remote_dma_fused([wtr], local_sem=T.sem.lw), "wdi", "", inc=0)
-    nw = len(topo.engines(core, T.cores[ask[0]]))
-    iota(T.tz[:], [[0, 8], [ZZ, 2]], "tz")
-
+    iota(T.i32[:], [[1, 24]], "i32")
+    iota(T.eh[:], [[33, 2], [4, 8]], "eh")
+    iota(T.isl[:], [[16, 9], [136, 2], [0, 8]], "isl", -16, -1)
     ms(T.hf[:], 0.5, "hf")
-    ms(T.one[0:1, :], 1.0, "one")
+    ms(T.zr[:], 0.0, "zr")
     ms(T.o1[:], 0, "o1z")
-    ts(T.bi[:, 0:1], T.pi[:], 2, 0x70, SHR, AND, "pi", "bi", grp="bi")
-    ts(T.bi[:, 1:2], T.pi[:], 2, 15, SHR, AND, "pi", "bi", grp="bi")
-    ts(T.bi[:, 2:3], T.pi[:], 64, None, AND, None, "pi", "bi", grp="bi")
-    ts(T.bi[:, 3:4], T.pi[:], 5, 1, SHR, AND, "pi", "bi", grp="bi")
-    ts(T.bi[:, 4:5], T.pi[:], 2, 1, SHR, AND, "pi", "bi", grp="bi")
-    ms(T.d0[:], 0.0, "d0")
-    ms(T.rf[:, 192:200], 0.0, "rfp")
-    cp(T.eq[:, 16:21], T.bi[:], "bi", "bf")
-    scan(pt[:, 0:32], T.hf[:], T.d0[:, 0:32], 2.0, A.mult, A.add, "hf d0", "pw")
-    op("t", lambda q: q.matmul(T.ps[:, 0:16], T.one[0:1, :], T.t2[0:1, :], True, False), "one t2", "", inc=0)
-    for q in range(N):
-        act(T.tabq[:, 32 * q:32 * q + 32], T.hf[:], "hf", "tabq", grp="tabq", scale=0.0, bias=-32.0 * q)
-    for n in (16, 32):
-        act(T.eh[:, 2 * n:4 * n], T.eh[:, 0:2 * n], "eh", "eh")
-        act(T.isl[:, n:2 * n], T.isl[:, 0:n], "isl", "isl", bias=float(n))
+    ms(T.n16[:], -1.0 / 16, "n16")
+    ms(T.d0[:, 0:1], 0.0, "d0z")
+    for k, (a, m) in enumerate(((2, 15), (2, 1), (2, 7), (3, 7), (0, 64))):
+        ts(T.bi[:, k:k + 1], T.pi[:], a, m, SHR, AND, "pi", "bi", grp="bi")
+    act(T.bf[:], T.bi[:], "bi", "bf")
+    ts(T.tri[:], T.i32[:, 0:16], pp, 1024.0, A.is_ge, A.mult, "bf i32", "tri")
+    ts(T.diag[:], T.i32[:, 0:16], pp, None, A.is_equal, None, "bf i32", "diag")
+    ts(T.lh[:], T.isl[:], pp, 0.0, A.add, A.is_equal, "isl bf", "lh")
+    act(T.ut[:, 0::2], T.eh[:], "eh bf", "ut", grp="ut", name="ute", bias=od)
+    ts(T.ut[:, 1::2], T.eh[:], od, T2 / 8 + 4, A.subtract, A.add, "eh bf", "ut", grp="ut", name="uto")
+    act(T.c256[:], T.i32[:, 0:8], "i32", "c256", scale=1.0 / 256)
+    act(T.i6[:], T.i32[:, 0:8], "i32", "i6", scale=6.0)
+    act(c16, pp, "bf", "c16", scale=-1.0, bias=16.0)
 
-    cp(T.wme[:], wdi, "wdi", "wme")
-    ts(c16, p16, -1.0, 16.0, A.mult, A.add, "bf", "c16")
-    cp(wu, T.wt[:], "wt", "wu")
-    act(T.d1[:], T.i16[:].indirect(T.wme[:]), "i16 wme bf", "d1", scale=p16)
-    act(T.d0[:, 1:33], T.i16[:].indirect(T.wme[:]), "i16 wme c16", "d0", scale=c16)
-    act(T.isl[:, 64:128], T.isl[:, 0:64], "isl", "isl", bias=64.0)
-    ts(T.tri[:], T.i16[:], p16, 1024.0, A.is_ge, A.mult, "bf i16", "tri")
-    ts(T.qi[:], T.wt[:], 1.0 / 32, -15.5 / 32, A.mult, A.add, "wt", "qi")
-    ts(T.utab[:, 0:128:2], T.eh[:, 0:128:2], od, None, A.add, None, "eh bf", "utab", grp="utab")
-    tt(T.z[:], T.tabq[:].indirect(wu), T.tri[:], A.add, "tabq wu tri", "z")
-    ts(T.nq[:], T.qi[:], -32.0, None, A.mult, None, "qi", "nq")
-    ts(T.utab[:, 1:128:2], T.eh[:, 1:128:2], od, None, A.subtract, None, "eh bf", "utab", grp="utab")
-    ts(T.diag[:], T.i16[:], p16, None, A.is_equal, None, "bf i16", "diag")
-    scan(T.xs[:], T.d0[:, 0:32], T.d1[:], 0.0, A.add, A.add, "d0 d1", "xs")
-    ts(T.eq[:, 0:16], T.z[:], T.nq[:], None, A.is_equal, None, "z nq", "eq")
-    tt(T.ud[:], T.utab[:].indirect(wu), T.diag[:], A.mult, "utab wu diag", "ud")
-    ts(T.o1[:, 17:33], T.xs[:, 16:32], 0.5, -HB - 0.25, A.mult, A.add, "xs o1z", "o1", grp="o1")
-    red(T.rk[:], T.eq[:, 0:17], "eq bf", "rk")
+    nw = send(T.wdi[:], T.wfar[:], "wq", "lw", ask[2], "wdi")
+    act(wme, T.wdi[:], "wdi", "wme")
+    act(T.msg[:, ask[1], 0:2], T.wdi[:], "wdi", "wm2")
+
+    act(qu, T.wt[:], "wt", "qu", scale=1.0 / 32, bias=-15.5 / 32)
+    act(q6, qu, "qu", "q6", scale=6.0)
+    tt(T.z[:], T.i6[:].indirect(qu), T.tri[:], A.add, "i6 qu tri", "z")
+    ts(T.eq[:, 0:16], T.z[:], q6, None, A.is_equal, None, "z q6", "eq")
+    red(T.key[:], T.eq[:], "eq q6", "key")
+    ts(T.bq[:], T.wt[:], 31, None, AND, None, "wt", "bq")
+    act(bu, T.bq[:], "bq", "bu")
+    tt(T.ud[:], T.ut[:].indirect(bu), T.diag[:], A.mult, "ut bu diag", "ud")
     red(T.u[:], T.ud[:], "ud", "u")
-    ts(T.o1[:, 1:17], T.xs[:, 0:16], 0.5, -0.25, A.mult, A.add, "xs o1z", "o1", grp="o1")
-    ts(T.lh[:], T.isl[:], T.rk[:], 8.0, A.is_equal, A.mult, "isl rk", "lh")
-    ts(T.rh[:], T.tabq[:, 0:128:8], T.nq[:], T.u[:], A.is_equal, A.mult, "tabq nq u", "rh")
-    op("t", lambda q: q.matmul(T.ps[:, 0:16], T.lh[:], T.rh[:], False, True), "lh rh", "ps")
-    ts(T.sq[:], T.nq[:], -1.5, T.rk[:], A.mult, A.add, "nq rk", "sq")
+    ts(T.rh[:], T.i32[:, 0:24], T.key[:], T.u[:], A.is_equal, A.mult, "i32 key u", "rh")
+    op("t", lambda q: q.matmul(T.ps[:, 0:12], T.lh[:, 16:144], T.rh[:, 0::2], True, False), "lh rh", "", inc=0)
+    op("t", lambda q: q.matmul(T.ps[:, 0:12], T.lh[:, 8:136], T.rh[:, 1::2], False, True), "lh rh", "ps")
+    act(T.msg[:, :, 2:5], T.ps[:, 0:12], "ps bf", "msg", scale=8.0, bias=c8)
+    nq = sum(send(T.msg[:, p, n:5], T.req[:, me, n:5], "rq", "lq", p, "msg wme wm2") for p, n in zip(ask, (0, 0, 2)))
+    book(1, "gq")
 
-    act(s8, pr, "bf", "col", grp="col", scale=2.0 ** -8 - 1.0, bias=1.0)
-    act(e1, pr, "bf", "col", grp="col", scale=-1.0, bias=1.0)
-    act(o8, pr, "bf", "col", grp="col", scale=256.0)
-    act(pt[:, 32:49], pt[:, 0:17], "pw", "pa", grp="pa", scale=65536.0)
-    act(pt[:, 81:96], pt[:, 17:32], "pw", "pa", grp="pa", scale=2.0 ** 32)
-    act(pt[:, 96:104], pt[:, 0:8], "pw col", "pt", grp="pt", scale=s8)
-    act(pt[:, 104:128], pt[:, 8:32], "pw col", "pt", grp="pt", scale=e1)
-    act(pt[:, 128:137], pt[:, 32:41], "pa col", "pt", grp="pt", scale=s8)
-    act(pt[:, 137:145], pt[:, 41:49], "pa col bf", "pt", grp="pt", scale=e1, bias=pr)
-    act(pt[:, 169:177], pt[:, 41:49], "pa col", "pt", grp="pt", scale=o8)
-    act(pt[:, 177:192], pt[:, 81:96], "pa col", "pt", grp="pt", scale=s8)
+    act(T.d0[:, 1:33], T.i32[:].indirect(wme), "i32 wme c16", "d0", scale=c16)
+    act(T.d1[:], T.i32[:].indirect(wme), "i32 wme bf", "d1", scale=pp)
+    scan(T.xs[:], T.d0[:, 0:32], T.d1[:], 0.0, A.add, A.add, "d0 d0z d1", "xs")
+    for h in range(2):
+        act(T.o1[:, 1 + 16 * h:17 + 16 * h], T.xs[:, 16 * h:16 * h + 16], "xs o1z", "o1", grp="o1", scale=0.5, bias=-0.25 - X * h)
 
-    cp(T.gw[:, 0:256], T.win[:].indirect(T.o1[:, 0:16]), "win wtail o1", "gwa")
-    act(T.gw[:, 256:544], T.win[:].indirect(T.o1[:, 16:34]), "win wtail o1", "gwb")
-    ts(T.msg[:], T.ps[:, 0:16], kk, None, A.add, None, "ps bf", "msgl")
-    nq = sum(send(T.msg[:, p, 0:3], T.req[:, me, 0:3], "rq", "lq", p, "msgl") for p in ask)
-    op("g", lambda q: q.sem_inc(T.sem.gq, 1), "", "", inc=0)
-    dma("s", T.dc[:, 0:DH], T.dic[:, 0:DH], "", "dc", grp="dc", ext=[("gq", 1)])
-    ts(T.sr[:, 0:1], T.sq[:], g16, None, A.subtract, None, "sq bf", "sr", grp="sr")
-    ts(T.sr[:, 1:2], T.sq[:], g16, 8.0, A.subtract, A.add, "sq bf", "sr", grp="sr")
-    act(T.walu[:], T.wall[:], "wdi", "walu", ext=[("wq", sum(arrivals(r) for r in tell))])
-    for a, b, v in ((49, 64, 1.0), (64, 81, 0.0), (145, 160, 1.0)):
-        act(pt[:, a:b], pt[:, 0:b - a], "pw", "pt", grp="pt", scale=0.0, bias=v)
-    act(T.wrep[:], T.i16[:].indirect(T.walu[:]), "i16 walu", "wrep")
-    act(T.zrep[:], T.tz[:].indirect(T.walu[:]), "tz walu", "zrep")
-    act(pt[:, 160:169], pt[:, 0:9], "pw", "pt", grp="pt", scale=0.0)
-    turn(T2, 0, 256, "gwa", "twa")
-    turn(T2 + 256, 256, 288, "gwb", "twb")
-    turn(0, 16, 512, "gwa gwb", "twa")
+    for n in range(3):
+        a, b = GW[n], GW[n + 1]
+        c = max(a - 2, 0)
+        act(T.gw[:, 16 * a:16 * b], T.win[:].indirect(T.o1[:, a:b]), "win wtail o1", "gw%d" % n)
+        turn(T2 + 16 * a, 16 * a, 16 * (b - a), "gw%d" % n, "tw%db" % n)
+        turn(16 * c, 16 * c + 16, 16 * (b - 2 - c), "gw%d gw%d tw0b" % (max(n - 1, 0), n), "tw%da" % n)
+    turned = "tw0a tw0b tw1a tw1b tw2a tw2b"
+    na = 0
+    for n, p in enumerate(tell):
+        act(T.rsp[:, p, :], T.tw[:].indirect(T.req[:, p, 2:5]), turned, "rsp%d" % n, ext=landed("rq", p))
+        na += send(T.rsp[:, p, :], T.ans[:, me, :], "an", "la", p, "rsp%d" % n)
+    book(2, "ga")
+    act(T.rf[:, 48 * me:48 * me + 48], T.tw[:].indirect(T.msg[:, me, 2:5]), turned + " msg", "rf", grp="rf", name="rfme")
 
-    def answer(p):
-        cp(T.rsp[:, p, :], T.tw[:].indirect(T.req[:, p, 0:3]), "twa twb", "rsp%d" % p, ext=[("rq%d" % p, arrivals(p))])
-        return send(T.rsp[:, p, :], T.ans[:, me, :], "an", "la", p, "rsp%d" % p)
-
-    tt(T.wdg[:], T.wrep[:].indirect(wu), T.diag[:], A.mult, "wrep wu diag", "wdg")
-    tt(T.zdg[:], T.zrep[:].indirect(wu), T.diag[:], A.mult, "zrep wu diag", "zdg")
-    act(T.wz[:, 0:16], T.wdg[:], "wdg", "wi", accum_out=T.wi[:])
-    act(T.wz[:, 16:32], T.zdg[:], "zdg", "zz", accum_out=T.zz[:])
-    act(T.cw[:], i8, "i16 wi", "cw", scale=T.wi[:])
-    act(T.k16[:], T.wi[:], "wi", "k16", scale=-1.0, bias=16.0)
-    act(T.zw[:, 0:1], T.zz[:], "zz wi", "zw0", bias=T.wi[:])
-    na = sum(answer(p) for p in tell)
-    op("g", lambda q: q.sem_inc(T.sem.ga, 1), "", "", inc=0)
-    dma("s", T.dc[:, DH:], T.dic[:, DH:], "", "dc", grp="dc", ext=[("ga", 1)])
+    scan(T.pw[:, 0:32], T.hf[:], T.zr[:], 2.0 ** 17, A.mult, A.add, "hf zr", "pw")
+    act(e1, pr, "bf", "e1", scale=-1.0, bias=1.0)
+    act(s8, pr, "bf", "s8", scale=2.0 ** -8 - 1.0, bias=1.0)
+    act(T.pw[:, 32:64], T.pw[:, 0:32], "pw s8", "pw2", scale=s8)
+    act(T.wz[:, 0::2], T.i32[:, 4:14:2], "i32 e1", "wz", grp="wz", scale=e1)
+    act(T.wz[:, 1::2], T.i32[:, 5:14:2], "i32 e1", "wz", grp="wz", scale=e1, bias=32.0)
+    act(T.cw[:], T.i32[:, 4:13], "i32 bf", "cw", scale=che)
     ts(T.po[:], T.cw[:], 15, None, AND, None, "cw", "po")
-    ts(T.fo[:], T.cw[:], 1, 0x78, SHR, AND, "cw", "fo")
-    act(T.x3[:], i8, "i16 k16", "x3", scale=0.0, bias=T.k16[:])
-    cp(T.rf[:, 48 * me:48 * me + 48], T.tw[:].indirect(T.msg[:, me, 0:3]), "twa twb msgl", "rf", grp="rf")
-    for t in range(2):
-        ts(T.x1[:, :, 4 * t:4 * t + 4], T.po[:], T.zw[:, 0:1], float(ZB * t), A.add, A.add, "po zw0", "x1", grp="x1")
-    ts(T.x2[:], T.po[:], T.zz[:], None, A.add, None, "po zz", "x2")
-    act(T.gb[:], pt[:, 0:32].indirect(T.x3[:]), "pw x3", "gb")
-    act(T.m1[:, 0:128], pt[:, ZB:].indirect(T.x1[:, 0, :]), "pa pt x1", "m10")
-    act(T.m1[:, 128:256], pt[:, ZB:].indirect(T.x1[:, 1, :]), "pa pt x1", "m11")
-    for t in range(2):
-        ts(T.o2[:, :, 4 * t:4 * t + 4], T.fo[:], T.sr[:, t:t + 1], None, A.add, None, "fo sr", "o2", grp="o2")
-    tt(T.ga[:], pt[:].indirect(T.x2[:]), T.gb[:], A.min, "pw pa pt x2 gb", "ga")
-    act(T.pn[:, 0:128], T.gb[:], "gb", "pn")
-    act(T.pm[:, 0:128], T.ga[:], "ga", "pm")
+    tt(T.xf[:], T.po[:], T.wz[:, 0:9], A.add, "po wz", "xf")
+    act(T.xe[:, 0:9], T.xf[:], "xf", "xe")
+    act(T.y16[:], T.pw[:].indirect(T.xe[:, 0:9]), "pw pw2 xe", "y16")
+    ts(T.tm[:, 0::2], yv, 1.0, None, A.max, None, "y16", "tm", grp="tm", name="tmx")
+    op("a", lambda q: q.activation(T.ta[:], yv, AF.Abs, bias=-0.5), "y16", "ta")
+    op("a", lambda q: q.activation(T.tm[:, 1::2], T.ta[:], AF.Relu, bias=32768.0, scale=-65536.0), "ta", "tm", grp="tm", name="tmy")
+    ts(T.pb[:, 0:72], zv, 1.0, None, A.is_gt, None, "y16", "pb")
+    tt(zv, T.pb[:, 0:72], yv, A.min, "pb y16", "td")
 
-    for p in ask:
-        cp(T.rf[:, 48 * p:48 * p + 48], T.ans[:, p, :], "", "rf", grp="rf", ext=[("an%d" % p, arrivals(p))])
+    act(T.wfu[:], T.wfar[:], "", "wfu", ext=landed("wq", tell[2]))
+    lists = [(T.req[:, p, 0:2], "", landed("rq", p)) for p in tell[:2]] + [(T.wfu[:], "wfu", []), (wme, "wme", [])]
+    for n, p in enumerate(tell + [me]):
+        act(T.wrep[:, 32 * p:32 * p + 32], T.i32[:].indirect(lists[n][0]), "i32 " + lists[n][1], "wrep", grp="wrep", scale=16.0,
+            name="wr%d" % n, ext=lists[n][2])
+    act(wu, T.wt[:], "wt", "wu")
+    tt(T.wdg[:], T.wrep[:].indirect(wu), T.diag[:], A.mult, "wrep wu diag", "wdg")
+    red(T.wi[:], T.wdg[:], "wdg", "wi")
+    act(b0, T.key[:], "key", "b0", scale=8.0, bias=-15.0 / 32)
+    act(b1, T.key[:], "key", "b1", scale=8.0, bias=17.0 / 32)
+    for t, b in enumerate((b0, b1)):
+        ts(T.o3[:, :, 4 * t:4 * t + 4], T.i32[:, 0:16:2], T.wi[:], t - 64.0, A.add, A.add, "i32 wi", "o3", grp="o3")
+        act(T.o2[:, :, 4 * t:4 * t + 4], T.c256[:], "c256 wi b%d" % t, "o2", scale=T.wi[:], bias=b, grp="o2")
+    act(T.o5[:], T.n16[:], "n16 wi", "o5", scale=T.wi[:], bias=16.0)
+    act(T.d2[:, 1::2], T.pw[:, 0:32].indirect(T.o5[:]), "pw o5", "d2f", scale=2.0 ** -40)
+    for h in range(2):
+        act(T.m1[:, 128 * h:128 * h + 128], T.tm[:].indirect(T.o3[:, h, :]), "tm o3", "m1%d" % h)
+        act(T.d2[:, 128 * h:128 * h + 128:2], T.y16[:].indirect(T.o3[:, h, 4:8]), "td o3", "d2%d" % h)
 
-    def step(k, h):
-        c, j = slice(128 * h, 128 * h + 128), slice(64 * h, 64 * h + 64)
-        ca, cb = slice(128 * h, 128 * h + 64), slice(128 * h + 64, 128 * h + 128)
-        if k == 0:
-            tt(T.ya[:, c], T.rf[:].indirect(T.o2[:, h, :]), T.m1[:, c], A.mult, "rf rfp o2 m1%d" % h, "ya%d" % h)
-        if k == 1:
-            ts(T.yb[:, c], T.ya[:, c], 0xFFF0, None, AND, None, "ya%d" % h, "yb%d" % h)
-        if k == 2:
-            tt(T.yc[:, j], T.yb[:, cb], T.pn[:, j], A.mult, "yb%d pn" % h, "yc%d" % h, grp="yc%d" % h)
-            tt(T.pc[:, j], T.yb[:, ca], T.pm[:, j], A.mult, "yb%d pm" % h, "yc%d" % h, grp="yc%d" % h)
-        if k == 3:
-            tt(T.yd[:, j], T.yc[:, j], T.pc[:, j], A.add, "yc%d" % h, "yd%d" % h)
-        if k == 4:
-            ts(T.cu[:, j], T.yd[:, j], -0.5 + 2.0 ** -12, None, A.add, None, "yd%d" % h, "cu%d" % h)
-
-    for k in range(5):
-        for h in range(2):
-            step(k, h)
+    for n, p in enumerate(ask):
+        act(T.rf[:, 48 * p:48 * p + 48], T.ans[:, p, :], "", "rf", grp="rf", name="rf%d" % n, ext=landed("an", p))
+    for h in range(2):
+        c = slice(128 * h, 128 * h + 128)
+        tt(T.ya[:, c], T.rf[:].indirect(T.o2[:, h, :]), T.m1[:, c], A.mult, "rf o2 m1%d" % h, "ya%d" % h)
+        for t in range(2):
+            ts(T.yb[:, 128 * h + t:128 * h + 128:2], T.ya[:, 128 * h + 64 * t:128 * h + 64 * t + 64], 0xFFF0, None, AND, None,
+               "ya%d" % h, "yb%d" % h, grp="yb%d" % h)
+        scan(T.sc[:, c], T.yb[:, c], T.d2[:, c], 0.0, A.add, A.mult, "yb%d d2%d d2f" % (h, h), "sc%d" % h)
+        act(T.cu[:, 64 * h:64 * h + 64], T.sc[:, 128 * h + 1:128 * h + 128:2], "sc%d" % h, "cu%d" % h, scale=2.0 ** 24, bias=FLOOR)
 
     for h, (a, b) in enumerate(CH):
         for c in range(8):
-            out = T.ob[:, 128 * a + c:128 * b:8]
-            src = T.dc[:].indirect(T.cu[:, 16 * c + a:16 * c + b])
-            if c >= 4:
-                cp(out, src, "dc cu1", "ov%d" % h, grp="ov%d" % h)
-            else:
-                act(out, src, "dc cu0", "oa%d" % h, grp="oa%d" % h)
-        dma("s", T.y[:, 128 * a:128 * b], T.ob[:, 128 * a:128 * b], "ov%d oa%d" % (h, h), "y", grp="y")
+            act(T.ob[:, 128 * a + c:128 * b:8], T.dc[:].indirect(T.cu[:, 16 * c + a:16 * c + b]),
+                "dc cu%d" % (c // 4), "ob%d" % h, grp="ob%d" % h, name="l%d%d" % (h, c))
+        dma("s", T.y[:, 128 * a:128 * b], T.ob[:, 128 * a:128 * b], "ob%d" % h, "y", grp="y")
     op("s", lambda q: None, "y", "", inc=0, ext=[("lq", nq), ("la", na), ("lw", nw)])
 
     emit(ops, {"g": g, "v": g.vector, "a": g.scalar, "s": g.sync, "t": g.tensor}, T)

from concourse.mybir import AluOpType as A, AxisListType, ActivationFunctionType as AF

N, S = 4, 2176
X, W0, WN = 512, 1536, 1664
T2 = 496
GW = (0, 6, 18, 34)
DC = (0, 1024, 2560, 4096)
CH = ((0, 10), (10, 16))

ORDER = {"v": "wtail d0z zr hf bi pw o1z bf n16 bq tri ute diag uto z bu po d1 eq ud xf key u xe xs lh rh o1 b0 c256 "
              "gw0 msg tmx pb tw0b tw1b tw0a tw1a tw2a tw2b wr0 rsp0 wdg rsp2 wi td o3 o5 m11 rf0 rf2 "
              "ya0 ya1 yb0 yb1 sc0 sc1 cu0 cu1 l03 l04 l05 l06 l11 l13 l14 l15 l16",
         "a": "wt win i6 wme qu e1 cw c16 q6 wz s8 d0 wm2 pw2 wu y16 gw1 gw2 wr3 ta b1 wfu tmy wr2 wr1 rsp1 rfme o2 m10 d20 "
              "rf1 d21 d2f"}

ONE, NIL = 1.0, 0.0
SCRATCH = {"msg": ("sbuf", [128, N, 8], "uint16"), "req": ("sbuf", [128, N, 8], "uint16"),
           "rsp": ("sbuf", [128, N, 48], "uint16"), "ans": ("sbuf", [128, N, 48], "uint16"),
           "o2": ("sbuf", [128, 2, 8], "uint16"), "o3": ("sbuf", [128, 2, 8], "uint16")}
for _t, _s in (("int32", "win:1664 wt:1 wdi:2 wfar:2 pi:1 bi:5 bq:1 cw:9 po:9 ya:256 yb:256"),
               ("uint16", "wfu:2 qu:2 wu:2 bu:2 o1:34 xe:10 o5:8 cu:128"),
               ("bfloat16", "dc:4096 ob:2048 isl:144 lh:144 rh:24"),
               ("float32", "i32:24 i6:8 wz:10 bf:5 y16:144 col:8 hf:32 zr:32 pw:64 xf:9 tri:16 diag:16 z:16 eq:17 u:1 key:1 "
                           "d0:33 d1:32 xs:32 eh:16 ut:32 ud:16 c256:8 n16:8 gw:544 tw:1040 rf:192 tm:144 ta:72 wrep:128 wdg:16 "
                           "wi:1 m1:256 d2:256 sc:256")):
    for _e in _s.split():
        SCRATCH[_e.split(":")[0]] = ("sbuf", [128, int(_e.split(":")[1])], _t)
for _e in ("ps", "pb"):
    SCRATCH[_e] = ("psum", [128, 512], "float32")
SEMAPHORES = (["s%d" % k for k in range(130)] + ["%s%d" % (s, k) for s in ("rq", "an", "wq") for k in range(N)]
              + ["lq", "la", "lw", "gq", "ga"])


def emit(ops, queues, T):
    last, readers, deps = {}, {}, []
    for n, o in enumerate(ops):
        d = set()
        for k in o["r"]:
            d.update(last.get(k, []))
        for k in o["w"]:
            if not (o["grp"] and all(ops[m]["grp"] == o["grp"] for m in last.get(k, []))):
                d.update(last.get(k, []))
                last[k] = []
            d.update(readers.get(k, []))
            readers[k] = []
        for k in o["r"]:
            readers.setdefault(k, []).append(n)
        for k in o["w"]:
            last.setdefault(k, []).append(n)
        d.discard(n)
        deps.append(d)
    key = [o["grp"] or ("op", n) for n, o in enumerate(ops)]
    need = set(key[m] for d in deps for m in d)
    total, sem = {}, {}
    for n, o in enumerate(ops):
        if key[n] in need:
            total[key[n]] = total.get(key[n], 0) + o["inc"]
            if key[n] not in sem:
                sem[key[n]] = T.sem["s%d" % len(sem)]

    def place(n):
        names = ORDER.get(ops[n]["q"], "").split()
        return (names.index(ops[n]["name"]) if ops[n]["name"] in names else len(names), n)

    done = {}
    for n in sorted(range(len(ops)), key=place):
        o = ops[n]
        q = queues[o["q"]]
        seen = done.setdefault(o["q"], set())
        for k in sorted(set(key[m] for m in deps[n]), key=str):
            if k not in seen and total[k]:
                q.wait_ge(sem[k], total[k])
                seen.add(k)
        for s, v in o["ext"]:
            if s not in seen:
                q.wait_ge(T.sem[s], v)
                seen.add(s)
        ins = o["f"](q)
        if key[n] in need and o["inc"]:
            ins.then_inc(sem[key[n]], o["inc"])


def rank_program(g, core, T, topo):
    me = T.rank_of(core)
    if me is None:
        return

    def near(a, b):
        return topo.same_plane(topo.chip(T.cores[a]), topo.chip(T.cores[b]))

    steps = sorted(range(1, N), key=lambda d: sum(near(r, (r + d) % N) for r in range(N)))
    ask = [(me + d) % N for d in steps]
    tell = [(me - d) % N for d in steps]
    ops = []

    def op(q, f, r, w, grp=None, inc=1, ext=(), name=None):
        ops.append({"q": q, "f": f, "r": r.split(), "w": w.split(), "grp": grp, "inc": inc, "ext": list(ext),
                    "name": name or w})

    def ts(out, in0, s1, s2, o0, o1, r, w, **kw):
        if o1 is None:
            op("v", lambda q: q.tensor_scalar(out, in0, s1, None, o0), r, w, **kw)
        else:
            op("v", lambda q: q.tensor_scalar(out, in0, s1, s2, o0, o1), r, w, **kw)

    def tt(out, a, b, o, r, w, **kw):
        op("v", lambda q: q.tensor_tensor(out, a, b, o), r, w, **kw)

    def ms(out, c, w):
        op("v", lambda q: q.memset(out, c), "", w)

    def red(out, a, r, w):
        op("v", lambda q: q.tensor_reduce(out, a, AxisListType.X, A.add), r, w)

    def scan(out, a, b, first, o0, o1, r, w, **kw):
        op("v", lambda q: q.tensor_tensor_scan(out, a, b, first, o0, o1), r, w, **kw)

    def turn(a, b, n, r, w, **kw):
        op("v", lambda q: q.transpose(T.tw[:, a:a + n], T.gw[:, b:b + n]), r, w, **kw)

    def act(out, a, r, w, scale=ONE, bias=NIL, **kw):
        plain = scale is ONE and bias is NIL
        if kw.get("name", w) not in ORDER["v"].split():
            op("a", lambda q: q.activation(out, a, AF.Copy if plain else AF.Identity, bias=bias, scale=scale), r, w, **kw)
        elif plain:
            op("v", lambda q: q.tensor_copy(out, a), r, w, **kw)
        else:
            ts(out, a, scale, bias, A.mult, A.add, r, w, **kw)
        ops[-1]["flex"] = True

    def dma(qn, out, a, r, w, **kw):
        op(qn, lambda q: q.dma_start(out, a), r, w, inc=16, **kw)

    def iota(out, pat, w, base=0, ch=0):
        op("g", lambda q: q.iota(out, pat, base, ch, allow_small_or_imprecise_dtypes=True), "", w)

    def send(src, dst, sem, local, p, r):
        rid, pid, _ = topo.addr(T.cores[p])
        op("g", lambda q: q.remote_dma(dst, src, T.sem["%s%d" % (sem, me)], T.sem[local], pid, rid,
                                       topo.mask(core, T.cores[p])), r, "", inc=0)
        return len(topo.engines(core, T.cores[p]))

    def landed(sem, p):
        return [("%s%d" % (sem, p), len(topo.engines(T.cores[p], core)))]

    def book(k, sem=None):
        if DC[k] < DC[k + 1]:
            if sem:
                op("g", lambda q: q.sem_inc(T.sem[sem], 1), "", "", inc=0)
            dma("s", T.dc[:, DC[k]:DC[k + 1]], T.dic[:, DC[k]:DC[k + 1]], "", "dc", grp="dc", ext=[(sem, 1)] if sem else [])

    pp, pr, c8, che, od = (T.bf[:, k:k + 1] for k in range(5))
    s8, b0, b1, e1, c16 = (T.col[:, k:k + 1] for k in range(5))
    SHR, AND = A.logical_shift_right, A.bitwise_and
    wme, wu, qu, bu, q6 = T.msg[:, ask[0], 0:2], T.wu[:, 0:1], T.qu[:, 0:1], T.bu[:, 0:1], T.eq[:, 16:17]
    yv, zv = T.y16[:, 0::2], T.y16[:, 1::2]
    FLOOR = -0.5 + 2.0 ** -12

    ms(T.win[:, W0:WN], 0, "wtail")
    dma("s", T.wdi[:], T.wd[:], "", "wdi")
    dma("a", T.wt[:], T.want[:], "", "wt")
    for k in range(8):
        dma("sa"[k < 4], T.win[k::16, 0:W0], T.strm[:, k:k + W0], "", "win", grp="win")
    for k in range(8):
        dma("s", T.win[8 + k::16, 0:WN - k], T.strm[:, X + k:S], "wtail", "win", grp="win")
    book(0)

    op("g", lambda q: q.iota(T.pi[:], [[0, 1]], 0, 4), "", "pi")
    iota(T.i32[:], [[1, 24]], "i32")
    iota(T.eh[:], [[33, 2], [4, 8]], "eh")
    iota(T.isl[:], [[16, 9], [136, 2], [0, 8]], "isl", -16, -1)
    ms(T.hf[:], 0.5, "hf")
    ms(T.zr[:], 0.0, "zr")
    ms(T.o1[:], 0, "o1z")
    ms(T.n16[:], -1.0 / 16, "n16")
    ms(T.d0[:, 0:1], 0.0, "d0z")
    for k, (a, m) in enumerate(((2, 15), (2, 1), (2, 7), (3, 7), (0, 64))):
        ts(T.bi[:, k:k + 1], T.pi[:], a, m, SHR, AND, "pi", "bi", grp="bi")
    act(T.bf[:], T.bi[:], "bi", "bf")
    ts(T.tri[:], T.i32[:, 0:16], pp, 1024.0, A.is_ge, A.mult, "bf i32", "tri")
    ts(T.diag[:], T.i32[:, 0:16], pp, None, A.is_equal, None, "bf i32", "diag")
    ts(T.lh[:], T.isl[:], pp, 0.0, A.add, A.is_equal, "isl bf", "lh")
    act(T.ut[:, 0::2], T.eh[:], "eh bf", "ut", grp="ut", name="ute", bias=od)
    ts(T.ut[:, 1::2], T.eh[:], od, T2 / 8 + 4, A.subtract, A.add, "eh bf", "ut", grp="ut", name="uto")
    act(T.c256[:], T.i32[:, 0:8], "i32", "c256", scale=1.0 / 256)
    act(T.i6[:], T.i32[:, 0:8], "i32", "i6", scale=6.0)
    act(c16, pp, "bf", "c16", scale=-1.0, bias=16.0)

    nw = send(T.wdi[:], T.wfar[:], "wq", "lw", ask[2], "wdi")
    act(wme, T.wdi[:], "wdi", "wme")
    act(T.msg[:, ask[1], 0:2], T.wdi[:], "wdi", "wm2")

    act(qu, T.wt[:], "wt", "qu", scale=1.0 / 32, bias=-15.5 / 32)
    act(q6, qu, "qu", "q6", scale=6.0)
    tt(T.z[:], T.i6[:].indirect(qu), T.tri[:], A.add, "i6 qu tri", "z")
    ts(T.eq[:, 0:16], T.z[:], q6, None, A.is_equal, None, "z q6", "eq")
    red(T.key[:], T.eq[:], "eq q6", "key")
    ts(T.bq[:], T.wt[:], 31, None, AND, None, "wt", "bq")
    act(bu, T.bq[:], "bq", "bu")
    tt(T.ud[:], T.ut[:].indirect(bu), T.diag[:], A.mult, "ut bu diag", "ud")
    red(T.u[:], T.ud[:], "ud", "u")
    ts(T.rh[:], T.i32[:, 0:24], T.key[:], T.u[:], A.is_equal, A.mult, "i32 key u", "rh")
    op("t", lambda q: q.matmul(T.ps[:, 0:12], T.lh[:, 16:144], T.rh[:, 0::2], True, False), "lh rh", "", inc=0)
    op("t", lambda q: q.matmul(T.ps[:, 0:12], T.lh[:, 8:136], T.rh[:, 1::2], False, True), "lh rh", "ps")
    act(T.msg[:, :, 2:5], T.ps[:, 0:12], "ps bf", "msg", scale=8.0, bias=c8)
    nq = sum(send(T.msg[:, p, n:5], T.req[:, me, n:5], "rq", "lq", p, "msg wme wm2") for p, n in zip(ask, (0, 0, 2)))
    book(1, "gq")

    act(T.d0[:, 1:33], T.i32[:].indirect(wme), "i32 wme c16", "d0", scale=c16)
    act(T.d1[:], T.i32[:].indirect(wme), "i32 wme bf", "d1", scale=pp)
    scan(T.xs[:], T.d0[:, 0:32], T.d1[:], 0.0, A.add, A.add, "d0 d0z d1", "xs")
    for h in range(2):
        act(T.o1[:, 1 + 16 * h:17 + 16 * h], T.xs[:, 16 * h:16 * h + 16], "xs o1z", "o1", grp="o1", scale=0.5, bias=-0.25 - X * h)

    for n in range(3):
        a, b = GW[n], GW[n + 1]
        c = max(a - 2, 0)
        act(T.gw[:, 16 * a:16 * b], T.win[:].indirect(T.o1[:, a:b]), "win wtail o1", "gw%d" % n)
        turn(T2 + 16 * a, 16 * a, 16 * (b - a), "gw%d" % n, "tw%db" % n)
        turn(16 * c, 16 * c + 16, 16 * (b - 2 - c), "gw%d gw%d tw0b" % (max(n - 1, 0), n), "tw%da" % n)
    turned = "tw0a tw0b tw1a tw1b tw2a tw2b"
    na = 0
    for n, p in enumerate(tell):
        act(T.rsp[:, p, :], T.tw[:].indirect(T.req[:, p, 2:5]), turned, "rsp%d" % n, ext=landed("rq", p))
        na += send(T.rsp[:, p, :], T.ans[:, me, :], "an", "la", p, "rsp%d" % n)
    book(2, "ga")
    act(T.rf[:, 48 * me:48 * me + 48], T.tw[:].indirect(T.msg[:, me, 2:5]), turned + " msg", "rf", grp="rf", name="rfme")

    scan(T.pw[:, 0:32], T.hf[:], T.zr[:], 2.0 ** 17, A.mult, A.add, "hf zr", "pw")
    act(e1, pr, "bf", "e1", scale=-1.0, bias=1.0)
    act(s8, pr, "bf", "s8", scale=2.0 ** -8 - 1.0, bias=1.0)
    act(T.pw[:, 32:64], T.pw[:, 0:32], "pw s8", "pw2", scale=s8)
    act(T.wz[:, 0::2], T.i32[:, 4:14:2], "i32 e1", "wz", grp="wz", scale=e1)
    act(T.wz[:, 1::2], T.i32[:, 5:14:2], "i32 e1", "wz", grp="wz", scale=e1, bias=32.0)
    act(T.cw[:], T.i32[:, 4:13], "i32 bf", "cw", scale=che)
    ts(T.po[:], T.cw[:], 15, None, AND, None, "cw", "po")
    tt(T.xf[:], T.po[:], T.wz[:, 0:9], A.add, "po wz", "xf")
    act(T.xe[:, 0:9], T.xf[:], "xf", "xe")
    act(T.y16[:], T.pw[:].indirect(T.xe[:, 0:9]), "pw pw2 xe", "y16")
    ts(T.tm[:, 0::2], yv, 1.0, None, A.max, None, "y16", "tm", grp="tm", name="tmx")
    op("a", lambda q: q.activation(T.ta[:], yv, AF.Abs, bias=-0.5), "y16", "ta")
    op("a", lambda q: q.activation(T.tm[:, 1::2], T.ta[:], AF.Relu, bias=32768.0, scale=-65536.0), "ta", "tm", grp="tm", name="tmy")
    ts(T.pb[:, 0:72], zv, 1.0, None, A.is_gt, None, "y16", "pb")
    tt(zv, T.pb[:, 0:72], yv, A.min, "pb y16", "td")

    act(T.wfu[:], T.wfar[:], "", "wfu", ext=landed("wq", tell[2]))
    lists = [(T.req[:, p, 0:2], "", landed("rq", p)) for p in tell[:2]] + [(T.wfu[:], "wfu", []), (wme, "wme", [])]
    for n, p in enumerate(tell + [me]):
        act(T.wrep[:, 32 * p:32 * p + 32], T.i32[:].indirect(lists[n][0]), "i32 " + lists[n][1], "wrep", grp="wrep", scale=16.0,
            name="wr%d" % n, ext=lists[n][2])
    act(wu, T.wt[:], "wt", "wu")
    tt(T.wdg[:], T.wrep[:].indirect(wu), T.diag[:], A.mult, "wrep wu diag", "wdg")
    red(T.wi[:], T.wdg[:], "wdg", "wi")
    act(b0, T.key[:], "key", "b0", scale=8.0, bias=-15.0 / 32)
    act(b1, T.key[:], "key", "b1", scale=8.0, bias=17.0 / 32)
    for t, b in enumerate((b0, b1)):
        ts(T.o3[:, :, 4 * t:4 * t + 4], T.i32[:, 0:16:2], T.wi[:], t - 64.0, A.add, A.add, "i32 wi", "o3", grp="o3")
        act(T.o2[:, :, 4 * t:4 * t + 4], T.c256[:], "c256 wi b%d" % t, "o2", scale=T.wi[:], bias=b, grp="o2")
    act(T.o5[:], T.n16[:], "n16 wi", "o5", scale=T.wi[:], bias=16.0)
    act(T.d2[:, 1::2], T.pw[:, 0:32].indirect(T.o5[:]), "pw o5", "d2f", scale=2.0 ** -40)
    for h in range(2):
        act(T.m1[:, 128 * h:128 * h + 128], T.tm[:].indirect(T.o3[:, h, :]), "tm o3", "m1%d" % h)
        act(T.d2[:, 128 * h:128 * h + 128:2], T.y16[:].indirect(T.o3[:, h, 4:8]), "td o3", "d2%d" % h)

    for n, p in enumerate(ask):
        act(T.rf[:, 48 * p:48 * p + 48], T.ans[:, p, :], "", "rf", grp="rf", name="rf%d" % n, ext=landed("an", p))
    for h in range(2):
        c = slice(128 * h, 128 * h + 128)
        tt(T.ya[:, c], T.rf[:].indirect(T.o2[:, h, :]), T.m1[:, c], A.mult, "rf o2 m1%d" % h, "ya%d" % h)
        for t in range(2):
            ts(T.yb[:, 128 * h + t:128 * h + 128:2], T.ya[:, 128 * h + 64 * t:128 * h + 64 * t + 64], 0xFFF0, None, AND, None,
               "ya%d" % h, "yb%d" % h, grp="yb%d" % h)
        scan(T.sc[:, c], T.yb[:, c], T.d2[:, c], 0.0, A.add, A.mult, "yb%d d2%d d2f" % (h, h), "sc%d" % h)
        act(T.cu[:, 64 * h:64 * h + 64], T.sc[:, 128 * h + 1:128 * h + 128:2], "sc%d" % h, "cu%d" % h, scale=2.0 ** 24, bias=FLOOR)

    for h, (a, b) in enumerate(CH):
        for c in range(8):
            act(T.ob[:, 128 * a + c:128 * b:8], T.dc[:].indirect(T.cu[:, 16 * c + a:16 * c + b]),
                "dc cu%d" % (c // 4), "ob%d" % h, grp="ob%d" % h, name="l%d%d" % (h, c))
        dma("s", T.y[:, 128 * a:128 * b], T.ob[:, 128 * a:128 * b], "ob%d" % h, "y", grp="y")
    op("s", lambda q: None, "y", "", inc=0, ext=[("lq", nq), ("la", na), ("lw", nw)])

    emit(ops, {"g": g, "v": g.vector, "a": g.scalar, "s": g.sync, "t": g.tensor}, T)
